import numpy as np
import ml_dtypes


def mxq(x, axis, fmt="e4m3"):
    dtype, down = {"e4m3": (ml_dtypes.float8_e4m3fn, 7), "e5m2": (ml_dtypes.float8_e5m2, 14)}[fmt]
    v = np.moveaxis(np.asarray(x, np.float32).astype(ml_dtypes.bfloat16).astype(np.float64), axis, -1)
    blocks = v.reshape(v.shape[:-1] + (-1, 32))
    amax = np.abs(blocks).max(-1, keepdims=True)
    byte = np.maximum(np.where(amax > 0, np.frexp(amax)[1] - 1 + 127, 0) - down, 1)
    scale = np.exp2(byte - 127.0)
    codes = (blocks / scale).astype(np.float32).astype(dtype).astype(np.float64)
    return np.moveaxis((codes * scale).reshape(v.shape), -1, axis)


WIDE = False


def mx_kscale(k):
    if not WIDE:
        return np.ones(k)
    levels = np.array([10, -10, 5, -5, 0])
    if k % 512:
        return np.exp2(np.random.permutation(np.resize(levels, k // 32))).repeat(32)
    a = np.empty((k // 512, 16))
    for p in range(k // 512):
        a[p, :8] = np.random.permutation(np.resize(levels, 8))
        for g in range(8):
            far = levels[np.abs(levels - a[p, g]) >= 10]
            a[p, g + 8] = far[np.random.randint(len(far))]
    return np.exp2(a.ravel()).repeat(32)


def f64(x):
    return np.asarray(x).astype(np.float64)


def striped(idx):
    return np.tile(idx.reshape(-1, 16).T, (8, 1)).astype(np.uint16)


def unstriped(offs):
    return offs[:16].T.reshape(-1).astype(np.int64)


def pack_weight(w):
    k, n = w.shape
    w = f64(np.asarray(w, np.float32).astype(ml_dtypes.bfloat16)).reshape(k // 32, 32, n)
    amax = np.abs(w).max(1)
    byte = np.clip(np.where(amax > 0, np.frexp(amax)[1] - 1 + 127 - 7, 1), 1, 254)
    scaled = (w * np.exp2(127.0 - byte)[:, None, :]).reshape(k, n).astype(np.float32)
    words = np.ascontiguousarray(scaled.reshape(k // 512, 128, 4, n).transpose(0, 1, 3, 2)).astype(ml_dtypes.float8_e4m3fn).view(np.uint8)
    return words, np.ascontiguousarray(byte.astype(np.uint8).reshape(k // 512, 16, n))


def unpack_weight(words, scales):
    g, p, n, _ = words.shape
    vals = np.ascontiguousarray(words).view(ml_dtypes.float8_e4m3fn).astype(np.float64) * np.repeat(np.exp2(scales.astype(np.float64) - 127.0), 8, axis=1)[..., None]
    return vals.transpose(0, 1, 3, 2).reshape(g * 512, n)


def relu(v):
    return np.maximum(v, 0.0)


K, T, S, V = 512, 2048, 512, 256


def setup_inputs():
    n = np.random.standard_normal
    s = mx_kscale(K)[:, None]
    packed_xT = pack_weight(n((K, T)) * s)
    packed_eT = pack_weight(n((K, T)) * s)
    return {
        "x_words": packed_xT[0],
        "x_scales": packed_xT[1],
        "e_words": packed_eT[0],
        "e_scales": packed_eT[1],
        "hT": (n((K, V)) / np.sqrt(K) / s).astype(np.float32),
        "offs": striped(np.random.permutation(T)[:S]),
    }


def reference(x_words, x_scales, e_words, e_scales, hT, offs):
    qp = relu(f64(hT))
    xq = unpack_weight(x_words, x_scales)[:, unstriped(offs)]
    qm = relu(-1.0 * f64(hT))
    e_offs = unpack_weight(e_words, e_scales)[:, unstriped(offs)]
    z = mxq(qm, 0, "e4m3").T @ e_offs
    y = (mxq(qp, 0, "e4m3").T @ xq) - z
    ex = np.exp(y - y.max(axis=1, keepdims=True))
    return ex / ex.sum(axis=1, keepdims=True)

@@ -1,0 +1,84 @@
+from contextlib import ExitStack
+
+import concourse.mybir as mybir
+
+K, T, S, V = 512, 2048, 512, 256
+FLOPS = 2 * 2 * K * V * S
+
+F32 = mybir.dt.float32
+BF16 = mybir.dt.bfloat16
+I32 = mybir.dt.int32
+U32 = mybir.dt.uint32
+U16 = mybir.dt.uint16
+U8 = mybir.dt.uint8
+FP8X4 = mybir.dt.float8_e4m3fn_x4
+ALU = mybir.AluOpType
+ACT = mybir.ActivationFunctionType
+AX = mybir.AxisListType
+P = 128
+
+
+def tile_picked_yquest_soft_p_kernel(tc, x_words, x_scales, e_words, e_scales, hT, offs, out):
+    nc = tc.nc
+    with ExitStack() as ctx:
+        keep = ctx.enter_context(tc.tile_pool(name="keep", bufs=1))
+        psum = ctx.enter_context(tc.psum_pool(name="psum", bufs=1))
+
+        offsets = keep.tile([P, S // 16], U16, name="offsets")
+        xs = keep.tile([P, T], U8, name="xs", align_bytes=64)
+        es = keep.tile([P, T], U8, name="es", align_bytes=64)
+        xw = keep.tile([P, T], I32, name="xw", align_bytes=64)
+        ew = keep.tile([P, T], I32, name="ew", align_bytes=64)
+        h = keep.tile([P, 4, V], F32, name="h", align_bytes=64)
+        xs_g = keep.tile([P, S], U8, name="xs_g", align_bytes=64)
+        es_g = keep.tile([P, S], U8, name="es_g", align_bytes=64)
+        xw_g = keep.tile([P, S], U32, name="xw_g", align_bytes=64)
+        ew_g = keep.tile([P, S], U32, name="ew_g", align_bytes=64)
+        qp = keep.tile([P, V, 4], BF16, name="qp", align_bytes=64)
+        qm = keep.tile([P, V, 4], BF16, name="qm", align_bytes=64)
+        qp_c = keep.tile([P, V], U32, name="qp_c", align_bytes=64)
+        qm_c = keep.tile([P, V], U32, name="qm_c", align_bytes=64)
+        qp_s = keep.tile([P, V], U8, name="qp_s", align_bytes=64)
+        qm_s = keep.tile([P, V], U8, name="qm_s", align_bytes=64)
+
+        nc.vector.memset(xs[:].bitcast(I32), 0)
+        nc.vector.memset(es[:].bitcast(I32), 0)
+        nc.sync.dma_start(offsets[:], offs)
+        for q in range(4):
+            nc.scalar.dma_start(out=xs[32 * q : 32 * q + 4, :].bitcast(I32), in_=x_scales[0, 4 * q : 4 * q + 4, :].bitcast(I32))
+        nc.sync.dma_start(out=h[:], in_=hT.rearrange("(p j) t -> p j t", j=4))
+        nc.sync.dma_start(out=xw[:], in_=x_words[0].rearrange("p n t -> p (n t)").bitcast(I32))
+        nc.sync.dma_start(out=ew[:], in_=e_words[0].rearrange("p n t -> p (n t)").bitcast(I32))
+        for q in range(4):
+            nc.gpsimd.dma_start(out=es[32 * q + 4 : 32 * q + 8, :].bitcast(I32), in_=e_scales[0, 4 * q : 4 * q + 4, :].bitcast(I32))
+
+        nc.vector.tensor_copy(xs_g[:], xs[:].indirect(offsets[:]))
+        hv = h[:].rearrange("p j (c i) -> p c j i", i=4)
+        nc.vector.tensor_scalar(qp[:].rearrange("p (c i) j -> p c j i", i=4), hv, -1.0, 0.0, ALU.mult, ALU.min)
+        nc.scalar.activation(qm[:].rearrange("p (c i) j -> p c j i", i=4), hv, ACT.Relu, scale=-1.0)
+        nc.vector.tensor_copy(xw_g[:], xw[:].bitcast(U32).indirect(offsets[:]))
+        nc.vector.quantize_mx(out=qp_c[:].bitcast(FP8X4), scales=qp_s[:], in_=qp[:].rearrange("p t j -> p (t j)"))
+        nc.vector.quantize_mx(out=qm_c[:].bitcast(FP8X4), scales=qm_s[:], in_=qm[:].rearrange("p t j -> p (t j)"))
+        nc.vector.tensor_copy(es_g[:], es[:].indirect(offsets[:]))
+        nc.vector.tensor_copy(ew_g[:], ew[:].bitcast(U32).indirect(offsets[:]))
+
+        acc = [psum.tile([P, S], F32, name=f"acc{b}") for b in range(2)]
+        for b in range(2):
+            c = slice(b * P, (b + 1) * P)
+            nc.tensor.matmul_mx(out=acc[b][:], lhsT=qp_c[:, c].bitcast(FP8X4), lhsT_scale=qp_s[:, c],
+                                rhs=xw_g[:].bitcast(FP8X4), rhs_scale=xs_g[:], start=True, stop=False)
+        for b in range(2):
+            c = slice(b * P, (b + 1) * P)
+            nc.tensor.matmul_mx(out=acc[b][:], lhsT=qm_c[:, c].bitcast(FP8X4), lhsT_scale=qm_s[:, c],
+                                rhs=ew_g[:].bitcast(FP8X4), rhs_scale=es_g[4:P, :], start=False, stop=True)
+        for b in range(2):
+            low = keep.tile([P, 1], F32, name=f"low{b}")
+            tot = keep.tile([P, 1], F32, name=f"tot{b}")
+            inv = keep.tile([P, 1], F32, name=f"inv{b}")
+            ex = keep.tile([P, S], F32, name=f"ex{b}")
+            res = keep.tile([P, S], F32, name=f"res{b}")
+            nc.vector.tensor_reduce(low[:], acc[b][:], AX.X, ALU.min)
+            nc.scalar.activation(ex[:], acc[b][:], ACT.Exp, bias=low[:], scale=-1.0, accum_out=tot[:])
+            nc.vector.reciprocal(inv[:], tot[:])
+            nc.vector.tensor_scalar(res[:], ex[:], inv[:], None, ALU.mult)
+            nc.sync.dma_start(out=out[b * P : (b + 1) * P, :], in_=res[:])

@@ -44,13 +44,13 @@ def tile_picked_yquest_soft_p_kernel(tc, x_words, x_scales, e_words, e_scales, h
         nc.vector.memset(xs[:].bitcast(I32), 0)
         nc.vector.memset(es[:].bitcast(I32), 0)
         nc.sync.dma_start(offsets[:], offs)
-        for q in range(4):
-            nc.scalar.dma_start(out=xs[32 * q : 32 * q + 4, :].bitcast(I32), in_=x_scales[0, 4 * q : 4 * q + 4, :].bitcast(I32))
         nc.sync.dma_start(out=h[:], in_=hT.rearrange("(p j) t -> p j t", j=4))
+        for r in range(4):
+            nc.sync.dma_start(out=xs[r:P:32, :].bitcast(I32), in_=x_scales[0, r:16:4, :].bitcast(I32))
         nc.sync.dma_start(out=xw[:], in_=x_words[0].rearrange("p n t -> p (n t)").bitcast(I32))
+        for r in range(4):
+            nc.sync.dma_start(out=es[4 + r : P : 32, :].bitcast(I32), in_=e_scales[0, r:16:4, :].bitcast(I32))
         nc.sync.dma_start(out=ew[:], in_=e_words[0].rearrange("p n t -> p (n t)").bitcast(I32))
-        for q in range(4):
-            nc.gpsimd.dma_start(out=es[32 * q + 4 : 32 * q + 8, :].bitcast(I32), in_=e_scales[0, 4 * q : 4 * q + 4, :].bitcast(I32))
 
         nc.vector.tensor_copy(xs_g[:], xs[:].indirect(offsets[:]))
         hv = h[:].rearrange("p j (c i) -> p c j i", i=4)

@@ -25,26 +25,20 @@ def tile_picked_yquest_soft_p_kernel(tc, x_words, x_scales, e_words, e_scales, h
         psum = ctx.enter_context(tc.psum_pool(name="psum", bufs=1))
 
         offsets = keep.tile([P, S // 16], U16, name="offsets")
-        xs = keep.tile([P, T], U8, name="xs", align_bytes=64)
+        xs = keep.tile([P, T], U8, name="xs", tag="xs", align_bytes=64)
         es = keep.tile([P, T], U8, name="es", align_bytes=64)
         xw = keep.tile([P, T], I32, name="xw", align_bytes=64)
         ew = keep.tile([P, T], I32, name="ew", align_bytes=64)
         h = keep.tile([P, 4, V], F32, name="h", align_bytes=64)
         xs_g = keep.tile([P, S], U8, name="xs_g", align_bytes=64)
         es_g = keep.tile([P, S], U8, name="es_g", align_bytes=64)
-        xw_g = keep.tile([P, S], U32, name="xw_g", align_bytes=64)
-        ew_g = keep.tile([P, S], U32, name="ew_g", align_bytes=64)
-        qp = keep.tile([P, V, 4], BF16, name="qp", align_bytes=64)
-        qm = keep.tile([P, V, 4], BF16, name="qm", align_bytes=64)
-        qp_c = keep.tile([P, V], U32, name="qp_c", align_bytes=64)
-        qm_c = keep.tile([P, V], U32, name="qm_c", align_bytes=64)
-        qp_s = keep.tile([P, V], U8, name="qp_s", align_bytes=64)
-        qm_s = keep.tile([P, V], U8, name="qm_s", align_bytes=64)
+        q = keep.tile([P, 2, V, 4], BF16, name="q", align_bytes=64)
+        q_s = keep.tile([P, 2, V], U8, name="q_s", align_bytes=64)
 
         nc.vector.memset(xs[:].bitcast(I32), 0)
         nc.vector.memset(es[:].bitcast(I32), 0)
-        nc.sync.dma_start(offsets[:], offs)
         nc.sync.dma_start(out=h[:], in_=hT.rearrange("(p j) t -> p j t", j=4))
+        nc.sync.dma_start(offsets[:], offs)
         for r in range(4):
             nc.sync.dma_start(out=xs[r:P:32, :].bitcast(I32), in_=x_scales[0, r:16:4, :].bitcast(I32))
         nc.sync.dma_start(out=xw[:], in_=x_words[0].rearrange("p n t -> p (n t)").bitcast(I32))
@@ -54,31 +48,38 @@ def tile_picked_yquest_soft_p_kernel(tc, x_words, x_scales, e_words, e_scales, h
 
         nc.vector.tensor_copy(xs_g[:], xs[:].indirect(offsets[:]))
         hv = h[:].rearrange("p j (c i) -> p c j i", i=4)
-        nc.vector.tensor_scalar(qp[:].rearrange("p (c i) j -> p c j i", i=4), hv, -1.0, 0.0, ALU.mult, ALU.min)
-        nc.scalar.activation(qm[:].rearrange("p (c i) j -> p c j i", i=4), hv, ACT.Relu, scale=-1.0)
+        nc.vector.tensor_scalar(q[:, 0].rearrange("p (c i) j -> p c j i", i=4), hv, -1.0, 0.0, ALU.mult, ALU.min)
+        nc.scalar.activation(q[:, 1].rearrange("p (c i) j -> p c j i", i=4), hv, ACT.Relu, scale=-1.0)
+        q_c = keep.tile([P, 2, V], U32, name="q_c", tag="xs", align_bytes=64)
+        nc.vector.quantize_mx(out=q_c[:].rearrange("p s t -> p (s t)").bitcast(FP8X4), scales=q_s[:].rearrange("p s t -> p (s t)"), in_=q[:].rearrange("p s t j -> p (s t j)"))
+        xw_g = keep.tile([P, S], U32, name="xw_g", align_bytes=64)
         nc.vector.tensor_copy(xw_g[:], xw[:].bitcast(U32).indirect(offsets[:]))
-        nc.vector.quantize_mx(out=qp_c[:].bitcast(FP8X4), scales=qp_s[:], in_=qp[:].rearrange("p t j -> p (t j)"))
-        nc.vector.quantize_mx(out=qm_c[:].bitcast(FP8X4), scales=qm_s[:], in_=qm[:].rearrange("p t j -> p (t j)"))
         nc.vector.tensor_copy(es_g[:], es[:].indirect(offsets[:]))
-        nc.vector.tensor_copy(ew_g[:], ew[:].bitcast(U32).indirect(offsets[:]))
+        ew_h = [keep.tile([P, S // 2], U32, name=f"ew_h{u}", align_bytes=64) for u in range(2)]
+        for u in range(2):
+            nc.vector.tensor_copy(ew_h[u][:], ew[:].bitcast(U32).indirect(offsets[:, 16 * u : 16 * u + 16]))
 
         acc = [psum.tile([P, S], F32, name=f"acc{b}") for b in range(2)]
         for b in range(2):
             c = slice(b * P, (b + 1) * P)
-            nc.tensor.matmul_mx(out=acc[b][:], lhsT=qp_c[:, c].bitcast(FP8X4), lhsT_scale=qp_s[:, c],
+            nc.tensor.matmul_mx(out=acc[b][:], lhsT=q_c[:, 0, c].bitcast(FP8X4), lhsT_scale=q_s[:, 0, c],
                                 rhs=xw_g[:].bitcast(FP8X4), rhs_scale=xs_g[:], start=True, stop=False)
-        for b in range(2):
-            c = slice(b * P, (b + 1) * P)
-            nc.tensor.matmul_mx(out=acc[b][:], lhsT=qm_c[:, c].bitcast(FP8X4), lhsT_scale=qm_s[:, c],
-                                rhs=ew_g[:].bitcast(FP8X4), rhs_scale=es_g[4:P, :], start=False, stop=True)
+        for u in range(2):
+            n = slice(u * S // 2, (u + 1) * S // 2)
+            for b in range(2):
+                c = slice(b * P, (b + 1) * P)
+                nc.tensor.matmul_mx(out=acc[b][:, n], lhsT=q_c[:, 1, c].bitcast(FP8X4), lhsT_scale=q_s[:, 1, c],
+                                    rhs=ew_h[u][:].bitcast(FP8X4), rhs_scale=es_g[4:P, n], start=False, stop=(u == 1))
         for b in range(2):
             low = keep.tile([P, 1], F32, name=f"low{b}")
             tot = keep.tile([P, 1], F32, name=f"tot{b}")
             inv = keep.tile([P, 1], F32, name=f"inv{b}")
             ex = keep.tile([P, S], F32, name=f"ex{b}")
-            res = keep.tile([P, S], F32, name=f"res{b}")
             nc.vector.tensor_reduce(low[:], acc[b][:], AX.X, ALU.min)
             nc.scalar.activation(ex[:], acc[b][:], ACT.Exp, bias=low[:], scale=-1.0, accum_out=tot[:])
             nc.vector.reciprocal(inv[:], tot[:])
-            nc.vector.tensor_scalar(res[:], ex[:], inv[:], None, ALU.mult)
-            nc.sync.dma_start(out=out[b * P : (b + 1) * P, :], in_=res[:])
+            for u in range(2):
+                n = slice(u * S // 2, (u + 1) * S // 2)
+                res = keep.tile([P, S // 2], F32, name=f"res{b}{u}")
+                nc.vector.tensor_scalar(res[:], ex[:, n], inv[:], None, ALU.mult)
+                nc.sync.dma_start(out=out[b * P : (b + 1) * P, n], in_=res[:])

@@ -59,27 +59,33 @@ def tile_picked_yquest_soft_p_kernel(tc, x_words, x_scales, e_words, e_scales, h
         for u in range(2):
             nc.vector.tensor_copy(ew_h[u][:], ew[:].bitcast(U32).indirect(offsets[:, 16 * u : 16 * u + 16]))
 
-        acc = [psum.tile([P, S], F32, name=f"acc{b}") for b in range(2)]
-        for b in range(2):
-            c = slice(b * P, (b + 1) * P)
-            nc.tensor.matmul_mx(out=acc[b][:], lhsT=q_c[:, 0, c].bitcast(FP8X4), lhsT_scale=q_s[:, 0, c],
-                                rhs=xw_g[:].bitcast(FP8X4), rhs_scale=xs_g[:], start=True, stop=False)
+        H = S // 2
+        acc = [[psum.tile([P, H], F32, name=f"acc{b}{u}") for u in range(2)] for b in range(2)]
         for u in range(2):
-            n = slice(u * S // 2, (u + 1) * S // 2)
+            n = slice(u * H, (u + 1) * H)
             for b in range(2):
                 c = slice(b * P, (b + 1) * P)
-                nc.tensor.matmul_mx(out=acc[b][:, n], lhsT=q_c[:, 1, c].bitcast(FP8X4), lhsT_scale=q_s[:, 1, c],
-                                    rhs=ew_h[u][:].bitcast(FP8X4), rhs_scale=es_g[4:P, n], start=False, stop=(u == 1))
+                nc.tensor.matmul_mx(out=acc[b][u][:], lhsT=q_c[:, 0, c].bitcast(FP8X4), lhsT_scale=q_s[:, 0, c],
+                                    rhs=xw_g[:, n].bitcast(FP8X4), rhs_scale=xs_g[:, n], start=True, stop=False)
+        for u in range(2):
+            n = slice(u * H, (u + 1) * H)
+            for b in range(2):
+                c = slice(b * P, (b + 1) * P)
+                nc.tensor.matmul_mx(out=acc[b][u][:], lhsT=q_c[:, 1, c].bitcast(FP8X4), lhsT_scale=q_s[:, 1, c],
+                                    rhs=ew_h[u][:].bitcast(FP8X4), rhs_scale=es_g[4:P, n], start=False, stop=True)
         for b in range(2):
+            low0 = keep.tile([P, 1], F32, name=f"low0{b}")
             low = keep.tile([P, 1], F32, name=f"low{b}")
             tot = keep.tile([P, 1], F32, name=f"tot{b}")
             inv = keep.tile([P, 1], F32, name=f"inv{b}")
+            neg = keep.tile([P, S], F32, name=f"neg{b}")
             ex = keep.tile([P, S], F32, name=f"ex{b}")
-            nc.vector.tensor_reduce(low[:], acc[b][:], AX.X, ALU.min)
-            nc.scalar.activation(ex[:], acc[b][:], ACT.Exp, bias=low[:], scale=-1.0, accum_out=tot[:])
+            nc.vector.tensor_scalar(neg[:, :H], acc[b][0][:], 1.0, None, ALU.mult, ALU.min, accum_out=low0[:])
+            nc.vector.tensor_scalar(neg[:, H:], acc[b][1][:], 1.0, low0[:], ALU.mult, ALU.min, accum_out=low[:])
+            nc.scalar.activation(ex[:], neg[:], ACT.Exp, bias=low[:], scale=-1.0, accum_out=tot[:])
             nc.vector.reciprocal(inv[:], tot[:])
             for u in range(2):
-                n = slice(u * S // 2, (u + 1) * S // 2)
-                res = keep.tile([P, S // 2], F32, name=f"res{b}{u}")
+                n = slice(u * H, (u + 1) * H)
+                res = keep.tile([P, H], F32, name=f"res{b}{u}")
                 nc.vector.tensor_scalar(res[:], ex[:, n], inv[:], None, ALU.mult)
                 nc.sync.dma_start(out=out[b * P : (b + 1) * P, n], in_=res[:])

@@ -36,25 +36,31 @@ def tile_picked_yquest_soft_p_kernel(tc, x_words, x_scales, e_words, e_scales, h
         q_s = keep.tile([P, 2, V], U8, name="q_s", align_bytes=64)
 
         nc.vector.memset(xs[:].bitcast(I32), 0)
-        nc.vector.memset(es[:].bitcast(I32), 0)
+        nc.gpsimd.memset(es[:].bitcast(I32), 0)
+        xs_m = keep.tile([P, S], U8, name="xs_m", align_bytes=64)
+        es_m = keep.tile([P, S], U8, name="es_m", align_bytes=64)
+        nc.vector.memset(xs_m[:].bitcast(I32), 0)
         nc.sync.dma_start(out=h[:], in_=hT.rearrange("(p j) t -> p j t", j=4))
         nc.sync.dma_start(offsets[:], offs)
-        for r in range(4):
-            nc.sync.dma_start(out=xs[r:P:32, :].bitcast(I32), in_=x_scales[0, r:16:4, :].bitcast(I32))
+        nc.sync.dma_start(out=xs[0:P:8, :].bitcast(I32), in_=x_scales[0].bitcast(I32))
+        nc.sync.dma_start(out=es[4:P:8, :].bitcast(I32), in_=e_scales[0].bitcast(I32))
         nc.sync.dma_start(out=xw[:], in_=x_words[0].rearrange("p n t -> p (n t)").bitcast(I32))
-        for r in range(4):
-            nc.sync.dma_start(out=es[4 + r : P : 32, :].bitcast(I32), in_=e_scales[0, r:16:4, :].bitcast(I32))
         nc.sync.dma_start(out=ew[:], in_=e_words[0].rearrange("p n t -> p (n t)").bitcast(I32))
 
         nc.vector.tensor_copy(xs_g[:], xs[:].indirect(offsets[:]))
+        nc.vector.tensor_copy(es_g[:], es[:].indirect(offsets[:]))
         hv = h[:].rearrange("p j (c i) -> p c j i", i=4)
         nc.vector.tensor_scalar(q[:, 0].rearrange("p (c i) j -> p c j i", i=4), hv, -1.0, 0.0, ALU.mult, ALU.min)
         nc.scalar.activation(q[:, 1].rearrange("p (c i) j -> p c j i", i=4), hv, ACT.Relu, scale=-1.0)
-        q_c = keep.tile([P, 2, V], U32, name="q_c", tag="xs", align_bytes=64)
+        for r in range(4):
+            nc.scalar.dma_start(out=xs_m[r:P:32, :].bitcast(I32), in_=xs_g[8 * r : P : 32, :].bitcast(I32))
+        q_c = keep.tile([P, 2, V], U32, name="q_c", align_bytes=64)
         nc.vector.quantize_mx(out=q_c[:].rearrange("p s t -> p (s t)").bitcast(FP8X4), scales=q_s[:].rearrange("p s t -> p (s t)"), in_=q[:].rearrange("p s t j -> p (s t j)"))
+        nc.vector.tensor_copy(es_m[:].bitcast(I32), es_g[:].bitcast(I32))
+        for r in range(1, 4):
+            nc.scalar.dma_start(out=es_m[4 + r : P : 32, :].bitcast(I32), in_=es_g[4 + 8 * r : P : 32, :].bitcast(I32))
         xw_g = keep.tile([P, S], U32, name="xw_g", align_bytes=64)
         nc.vector.tensor_copy(xw_g[:], xw[:].bitcast(U32).indirect(offsets[:]))
-        nc.vector.tensor_copy(es_g[:], es[:].indirect(offsets[:]))
         ew_h = [keep.tile([P, S // 2], U32, name=f"ew_h{u}", align_bytes=64) for u in range(2)]
         for u in range(2):
             nc.vector.tensor_copy(ew_h[u][:], ew[:].bitcast(U32).indirect(offsets[:, 16 * u : 16 * u + 16]))
@@ -66,13 +72,13 @@ def tile_picked_yquest_soft_p_kernel(tc, x_words, x_scales, e_words, e_scales, h
             for b in range(2):
                 c = slice(b * P, (b + 1) * P)
                 nc.tensor.matmul_mx(out=acc[b][u][:], lhsT=q_c[:, 0, c].bitcast(FP8X4), lhsT_scale=q_s[:, 0, c],
-                                    rhs=xw_g[:, n].bitcast(FP8X4), rhs_scale=xs_g[:, n], start=True, stop=False)
+                                    rhs=xw_g[:, n].bitcast(FP8X4), rhs_scale=xs_m[:, n], start=True, stop=False)
         for u in range(2):
             n = slice(u * H, (u + 1) * H)
             for b in range(2):
                 c = slice(b * P, (b + 1) * P)
                 nc.tensor.matmul_mx(out=acc[b][u][:], lhsT=q_c[:, 1, c].bitcast(FP8X4), lhsT_scale=q_s[:, 1, c],
-                                    rhs=ew_h[u][:].bitcast(FP8X4), rhs_scale=es_g[4:P, n], start=False, stop=True)
+                                    rhs=ew_h[u][:].bitcast(FP8X4), rhs_scale=es_m[4:P, n], start=False, stop=True)
         for b in range(2):
             low0 = keep.tile([P, 1], F32, name=f"low0{b}")
             low = keep.tile([P, 1], F32, name=f"low{b}")

@@ -27,7 +27,7 @@ def tile_picked_yquest_soft_p_kernel(tc, x_words, x_scales, e_words, e_scales, h
         offsets = keep.tile([P, S // 16], U16, name="offsets")
         xs = keep.tile([P, T], U8, name="xs", tag="xs", align_bytes=64)
         es = keep.tile([P, T], U8, name="es", align_bytes=64)
-        xw = keep.tile([P, T], I32, name="xw", align_bytes=64)
+        xw = keep.tile([P, T], I32, name="xw", tag="xw", align_bytes=64)
         ew = keep.tile([P, T], I32, name="ew", align_bytes=64)
         h = keep.tile([P, 4, V], F32, name="h", align_bytes=64)
         xs_g = keep.tile([P, S], U8, name="xs_g", align_bytes=64)
@@ -35,32 +35,35 @@ def tile_picked_yquest_soft_p_kernel(tc, x_words, x_scales, e_words, e_scales, h
         q = keep.tile([P, 2, V, 4], BF16, name="q", align_bytes=64)
         q_s = keep.tile([P, 2, V], U8, name="q_s", align_bytes=64)
 
-        nc.vector.memset(xs[:].bitcast(I32), 0)
-        nc.gpsimd.memset(es[:].bitcast(I32), 0)
-        xs_m = keep.tile([P, S], U8, name="xs_m", align_bytes=64)
         es_m = keep.tile([P, S], U8, name="es_m", align_bytes=64)
-        nc.vector.memset(xs_m[:].bitcast(I32), 0)
+        qm = keep.tile([P, V, 4], BF16, name="qm", align_bytes=64)
+        q_c = keep.tile([P, 2, V], U32, name="q_c", align_bytes=64)
+        nc.vector.memset(es[:].bitcast(I32), 0)
+        nc.gpsimd.memset(xs[:].bitcast(I32), 0)
+        nc.vector.memset(es_m[:].bitcast(I32), 0)
         nc.sync.dma_start(out=h[:], in_=hT.rearrange("(p j) t -> p j t", j=4))
         nc.sync.dma_start(offsets[:], offs)
-        nc.sync.dma_start(out=xs[0:P:8, :].bitcast(I32), in_=x_scales[0].bitcast(I32))
         nc.sync.dma_start(out=es[4:P:8, :].bitcast(I32), in_=e_scales[0].bitcast(I32))
+        for r in range(4):
+            nc.sync.dma_start(out=xs[r:P:32, :].bitcast(I32), in_=x_scales[0, r:16:4, :].bitcast(I32))
         nc.sync.dma_start(out=xw[:], in_=x_words[0].rearrange("p n t -> p (n t)").bitcast(I32))
         nc.sync.dma_start(out=ew[:], in_=e_words[0].rearrange("p n t -> p (n t)").bitcast(I32))
 
-        nc.vector.tensor_copy(xs_g[:], xs[:].indirect(offsets[:]))
         nc.vector.tensor_copy(es_g[:], es[:].indirect(offsets[:]))
-        hv = h[:].rearrange("p j (c i) -> p c j i", i=4)
-        nc.vector.tensor_scalar(q[:, 0].rearrange("p (c i) j -> p c j i", i=4), hv, -1.0, 0.0, ALU.mult, ALU.min)
-        nc.scalar.activation(q[:, 1].rearrange("p (c i) j -> p c j i", i=4), hv, ACT.Relu, scale=-1.0)
+        nc.vector.tensor_copy(xs_g[:], xs[:].indirect(offsets[:]))
         for r in range(4):
-            nc.scalar.dma_start(out=xs_m[r:P:32, :].bitcast(I32), in_=xs_g[8 * r : P : 32, :].bitcast(I32))
-        q_c = keep.tile([P, 2, V], U32, name="q_c", align_bytes=64)
-        nc.vector.quantize_mx(out=q_c[:].rearrange("p s t -> p (s t)").bitcast(FP8X4), scales=q_s[:].rearrange("p s t -> p (s t)"), in_=q[:].rearrange("p s t j -> p (s t j)"))
-        nc.vector.tensor_copy(es_m[:].bitcast(I32), es_g[:].bitcast(I32))
-        for r in range(1, 4):
-            nc.scalar.dma_start(out=es_m[4 + r : P : 32, :].bitcast(I32), in_=es_g[4 + 8 * r : P : 32, :].bitcast(I32))
+            nc.sync.dma_start(out=es_m[4 + r : P : 32, :].bitcast(I32), in_=es_g[4 + 8 * r : P : 32, :].bitcast(I32))
+        hv = h[:].rearrange("p j (c i) -> p c j i", i=4)
+        weave = lambda ap: ap.rearrange("p (c i) j -> p c j i", i=4)
+        flat = lambda ap: ap.rearrange("p t j -> p (t j)")
+        nc.scalar.activation(weave(q[:, 0]), hv, ACT.Relu)
+        nc.scalar.activation(weave(qm[:]), hv, ACT.Relu, scale=-1.0)
+        nc.scalar.activation(flat(q[:, 1]), flat(qm[:]), ACT.Copy, scale=-1.0)
+        nc.vector.quantize_mx(out=q_c[:, 0].bitcast(FP8X4), scales=q_s[:, 0], in_=flat(q[:, 0]))
         xw_g = keep.tile([P, S], U32, name="xw_g", align_bytes=64)
         nc.vector.tensor_copy(xw_g[:], xw[:].bitcast(U32).indirect(offsets[:]))
+        qm_c = keep.tile([P, V], U32, name="qm_c", tag="xw", align_bytes=64)
+        nc.vector.quantize_mx(out=qm_c[:].bitcast(FP8X4), scales=q_s[:, 1], in_=flat(q[:, 1]))
         ew_h = [keep.tile([P, S // 2], U32, name=f"ew_h{u}", align_bytes=64) for u in range(2)]
         for u in range(2):
             nc.vector.tensor_copy(ew_h[u][:], ew[:].bitcast(U32).indirect(offsets[:, 16 * u : 16 * u + 16]))
@@ -72,26 +75,34 @@ def tile_picked_yquest_soft_p_kernel(tc, x_words, x_scales, e_words, e_scales, h
             for b in range(2):
                 c = slice(b * P, (b + 1) * P)
                 nc.tensor.matmul_mx(out=acc[b][u][:], lhsT=q_c[:, 0, c].bitcast(FP8X4), lhsT_scale=q_s[:, 0, c],
-                                    rhs=xw_g[:, n].bitcast(FP8X4), rhs_scale=xs_m[:, n], start=True, stop=False)
+                                    rhs=xw_g[:, n].bitcast(FP8X4), rhs_scale=xs_g[:, n], start=True, stop=False)
         for u in range(2):
             n = slice(u * H, (u + 1) * H)
             for b in range(2):
                 c = slice(b * P, (b + 1) * P)
-                nc.tensor.matmul_mx(out=acc[b][u][:], lhsT=q_c[:, 1, c].bitcast(FP8X4), lhsT_scale=q_s[:, 1, c],
+                nc.tensor.matmul_mx(out=acc[b][u][:], lhsT=qm_c[:, c].bitcast(FP8X4), lhsT_scale=q_s[:, 1, c],
                                     rhs=ew_h[u][:].bitcast(FP8X4), rhs_scale=es_m[4:P, n], start=False, stop=True)
+        col = lambda name: keep.tile([P, 1], F32, name=name)
+        neg = [keep.tile([P, S], F32, name=f"neg{b}") for b in range(2)]
+        ex = [keep.tile([P, S], F32, name=f"ex{b}") for b in range(2)]
+        low0, low, inv = ([col(f"{name}{b}") for b in range(2)] for name in ("low0", "low", "inv"))
         for b in range(2):
-            low0 = keep.tile([P, 1], F32, name=f"low0{b}")
-            low = keep.tile([P, 1], F32, name=f"low{b}")
-            tot = keep.tile([P, 1], F32, name=f"tot{b}")
-            inv = keep.tile([P, 1], F32, name=f"inv{b}")
-            neg = keep.tile([P, S], F32, name=f"neg{b}")
-            ex = keep.tile([P, S], F32, name=f"ex{b}")
-            nc.vector.tensor_scalar(neg[:, :H], acc[b][0][:], 1.0, None, ALU.mult, ALU.min, accum_out=low0[:])
-            nc.vector.tensor_scalar(neg[:, H:], acc[b][1][:], 1.0, low0[:], ALU.mult, ALU.min, accum_out=low[:])
-            nc.scalar.activation(ex[:], neg[:], ACT.Exp, bias=low[:], scale=-1.0, accum_out=tot[:])
-            nc.vector.reciprocal(inv[:], tot[:])
-            for u in range(2):
-                n = slice(u * H, (u + 1) * H)
-                res = keep.tile([P, H], F32, name=f"res{b}{u}")
-                nc.vector.tensor_scalar(res[:], ex[:, n], inv[:], None, ALU.mult)
-                nc.sync.dma_start(out=out[b * P : (b + 1) * P, n], in_=res[:])
+            nc.vector.tensor_scalar(neg[b][:, :H], acc[b][0][:], -1.0, None, ALU.mult, ALU.min, accum_out=low0[b][:])
+            nc.vector.tensor_scalar(neg[b][:, H:], acc[b][1][:], -1.0, low0[b][:], ALU.mult, ALU.min, accum_out=low[b][:])
+        res = [[keep.tile([P, H], F32, name=f"res{b}{u}") for u in range(2)] for b in range(2)]
+        early, late, shift, tot0, tot1 = (col(name) for name in ("early", "late", "shift", "tot0", "tot1"))
+        nc.scalar.activation(ex[0][:, :H], neg[0][:, :H], ACT.Exp, bias=low0[0][:], scale=-1.0, accum_out=early[:])
+        nc.scalar.activation(shift[:], low0[0][:], ACT.Exp, bias=low[0][:], scale=-1.0)
+        nc.scalar.activation(ex[0][:, H:], neg[0][:, H:], ACT.Exp, bias=low[0][:], scale=-1.0, accum_out=late[:])
+        nc.vector.tensor_scalar(tot0[:], early[:], shift[:], late[:], ALU.mult, ALU.add)
+        nc.vector.reciprocal(inv[0][:], tot0[:])
+        nc.vector.tensor_scalar(res[0][0][:], ex[0][:, :H], shift[:], inv[0][:], ALU.mult, ALU.mult)
+        nc.sync.dma_start(out=out[:P, :H], in_=res[0][0][:])
+        nc.vector.tensor_scalar(res[0][1][:], ex[0][:, H:], inv[0][:], None, ALU.mult)
+        nc.sync.dma_start(out=out[:P, H:], in_=res[0][1][:])
+        nc.scalar.activation(ex[1][:], neg[1][:], ACT.Exp, bias=low[1][:], scale=-1.0, accum_out=tot1[:])
+        nc.vector.reciprocal(inv[1][:], tot1[:])
+        nc.vector.tensor_scalar(res[1][0][:], ex[1][:, :H], inv[1][:], None, ALU.mult)
+        nc.sync.dma_start(out=out[P:, :H], in_=res[1][0][:])
+        nc.scalar.activation(res[1][1][:], ex[1][:, H:], ACT.Copy, scale=inv[1][:])
+        nc.scalar.dma_start(out=out[P:, H:], in_=res[1][1][:])

@@ -38,12 +38,12 @@ def tile_picked_yquest_soft_p_kernel(tc, x_words, x_scales, e_words, e_scales, h
         es_m = keep.tile([P, S], U8, name="es_m", align_bytes=64)
         qm = keep.tile([P, V, 4], BF16, name="qm", align_bytes=64)
         q_c = keep.tile([P, 2, V], U32, name="q_c", align_bytes=64)
-        nc.vector.memset(es[:].bitcast(I32), 0)
-        nc.gpsimd.memset(xs[:].bitcast(I32), 0)
+        nc.vector.memset(xs[:].bitcast(I32), 0)
+        nc.vector.memset(es[: P - 16, :].bitcast(I32), 0)
         nc.vector.memset(es_m[:].bitcast(I32), 0)
         nc.sync.dma_start(out=h[:], in_=hT.rearrange("(p j) t -> p j t", j=4))
         nc.sync.dma_start(offsets[:], offs)
-        nc.sync.dma_start(out=es[4:P:8, :].bitcast(I32), in_=e_scales[0].bitcast(I32))
+        nc.sync.dma_start(out=es[P - 16 :, :].bitcast(I32), in_=e_scales[0].bitcast(I32))
         for r in range(4):
             nc.sync.dma_start(out=xs[r:P:32, :].bitcast(I32), in_=x_scales[0, r:16:4, :].bitcast(I32))
         nc.sync.dma_start(out=xw[:], in_=x_words[0].rearrange("p n t -> p (n t)").bitcast(I32))
@@ -52,7 +52,7 @@ def tile_picked_yquest_soft_p_kernel(tc, x_words, x_scales, e_words, e_scales, h
         nc.vector.tensor_copy(es_g[:], es[:].indirect(offsets[:]))
         nc.vector.tensor_copy(xs_g[:], xs[:].indirect(offsets[:]))
         for r in range(4):
-            nc.sync.dma_start(out=es_m[4 + r : P : 32, :].bitcast(I32), in_=es_g[4 + 8 * r : P : 32, :].bitcast(I32))
+            nc.sync.dma_start(out=es_m[4 + r : P : 32, :].bitcast(I32), in_=es_g[P - 16 + r : P : 4, :].bitcast(I32))
         hv = h[:].rearrange("p j (c i) -> p c j i", i=4)
         weave = lambda ap: ap.rearrange("p (c i) j -> p c j i", i=4)
         flat = lambda ap: ap.rearrange("p t j -> p (t j)")
@@ -105,4 +105,4 @@ def tile_picked_yquest_soft_p_kernel(tc, x_words, x_scales, e_words, e_scales, h
         nc.vector.tensor_scalar(res[1][0][:], ex[1][:, :H], inv[1][:], None, ALU.mult)
         nc.sync.dma_start(out=out[P:, :H], in_=res[1][0][:])
         nc.scalar.activation(res[1][1][:], ex[1][:, H:], ACT.Copy, scale=inv[1][:])
-        nc.scalar.dma_start(out=out[P:, H:], in_=res[1][1][:])
+        nc.sync.dma_start(out=out[P:, H:], in_=res[1][1][:])

@@ -14,95 +14,103 @@ U8 = mybir.dt.uint8
 FP8X4 = mybir.dt.float8_e4m3fn_x4
 ALU = mybir.AluOpType
 ACT = mybir.ActivationFunctionType
-AX = mybir.AxisListType
+
 P = 128
+PACK = 4
+GROUP = 32
+BLOCKS = K // 32
+HALF = S // 2
+E_ROW = 4
+STAGE = P - BLOCKS
 
 
 def tile_picked_yquest_soft_p_kernel(tc, x_words, x_scales, e_words, e_scales, hT, offs, out):
     nc = tc.nc
+    halves = [slice(u * HALF, (u + 1) * HALF) for u in range(2)]
+    queries = [slice(b * P, (b + 1) * P) for b in range(V // P)]
+
+    def woven(ap):
+        return ap.rearrange("p (c i) j -> p c j i", i=PACK)
+
+    def flat(ap):
+        return ap.rearrange("p t j -> p (t j)")
+
     with ExitStack() as ctx:
         keep = ctx.enter_context(tc.tile_pool(name="keep", bufs=1))
         psum = ctx.enter_context(tc.psum_pool(name="psum", bufs=1))
 
         offsets = keep.tile([P, S // 16], U16, name="offsets")
-        xs = keep.tile([P, T], U8, name="xs", tag="xs", align_bytes=64)
-        es = keep.tile([P, T], U8, name="es", align_bytes=64)
-        xw = keep.tile([P, T], I32, name="xw", tag="xw", align_bytes=64)
-        ew = keep.tile([P, T], I32, name="ew", align_bytes=64)
-        h = keep.tile([P, 4, V], F32, name="h", align_bytes=64)
-        xs_g = keep.tile([P, S], U8, name="xs_g", align_bytes=64)
-        es_g = keep.tile([P, S], U8, name="es_g", align_bytes=64)
-        q = keep.tile([P, 2, V, 4], BF16, name="q", align_bytes=64)
-        q_s = keep.tile([P, 2, V], U8, name="q_s", align_bytes=64)
+        x_scale_table = keep.tile([P, T], U8, name="x_scale_table", align_bytes=64)
+        e_scale_table = keep.tile([P, T], U8, name="e_scale_table", align_bytes=64)
+        x_word_table = keep.tile([P, T], I32, name="x_word_table", tag="x_words_then_qm_codes", align_bytes=64)
+        e_word_table = keep.tile([P, T], I32, name="e_word_table", align_bytes=64)
+        h = keep.tile([P, PACK, V], F32, name="h", align_bytes=64)
+        x_scale_picked = keep.tile([P, S], U8, name="x_scale_picked", align_bytes=64)
+        e_scale_picked = keep.tile([P, S], U8, name="e_scale_picked", align_bytes=64)
+        e_scale_placed = keep.tile([P, S], U8, name="e_scale_placed", align_bytes=64)
+        qp = keep.tile([P, V, PACK], BF16, name="qp", align_bytes=64)
+        qm = keep.tile([P, V, PACK], BF16, name="qm", align_bytes=64)
+        qm_negated = keep.tile([P, V, PACK], BF16, name="qm_negated", align_bytes=64)
+        qp_codes = keep.tile([P, V], U32, name="qp_codes", align_bytes=64)
+        qp_scales = keep.tile([P, V], U8, name="qp_scales", align_bytes=64)
+        qm_scales = keep.tile([P, V], U8, name="qm_scales", align_bytes=64)
 
-        es_m = keep.tile([P, S], U8, name="es_m", align_bytes=64)
-        qm = keep.tile([P, V, 4], BF16, name="qm", align_bytes=64)
-        q_c = keep.tile([P, 2, V], U32, name="q_c", align_bytes=64)
-        nc.vector.memset(xs[:].bitcast(I32), 0)
-        nc.vector.memset(es[: P - 16, :].bitcast(I32), 0)
-        nc.vector.memset(es_m[:].bitcast(I32), 0)
-        nc.sync.dma_start(out=h[:], in_=hT.rearrange("(p j) t -> p j t", j=4))
+        nc.vector.memset(x_scale_table[:].bitcast(I32), 0)
+        nc.vector.memset(e_scale_table[:STAGE, :].bitcast(I32), 0)
+        nc.vector.memset(e_scale_placed[:].bitcast(I32), 0)
+
+        nc.sync.dma_start(out=h[:], in_=hT.rearrange("(p j) t -> p j t", j=PACK))
         nc.sync.dma_start(offsets[:], offs)
-        nc.sync.dma_start(out=es[P - 16 :, :].bitcast(I32), in_=e_scales[0].bitcast(I32))
-        for r in range(4):
-            nc.sync.dma_start(out=xs[r:P:32, :].bitcast(I32), in_=x_scales[0, r:16:4, :].bitcast(I32))
-        nc.sync.dma_start(out=xw[:], in_=x_words[0].rearrange("p n t -> p (n t)").bitcast(I32))
-        nc.sync.dma_start(out=ew[:], in_=e_words[0].rearrange("p n t -> p (n t)").bitcast(I32))
+        nc.sync.dma_start(out=e_scale_table[STAGE:, :].bitcast(I32), in_=e_scales[0].bitcast(I32))
+        for r in range(PACK):
+            nc.sync.dma_start(out=x_scale_table[r:P:GROUP, :].bitcast(I32), in_=x_scales[0, r:BLOCKS:PACK, :].bitcast(I32))
+        nc.sync.dma_start(out=x_word_table[:], in_=x_words[0].rearrange("p n t -> p (n t)").bitcast(I32))
+        nc.sync.dma_start(out=e_word_table[:], in_=e_words[0].rearrange("p n t -> p (n t)").bitcast(I32))
 
-        nc.vector.tensor_copy(es_g[:], es[:].indirect(offsets[:]))
-        nc.vector.tensor_copy(xs_g[:], xs[:].indirect(offsets[:]))
-        for r in range(4):
-            nc.sync.dma_start(out=es_m[4 + r : P : 32, :].bitcast(I32), in_=es_g[P - 16 + r : P : 4, :].bitcast(I32))
-        hv = h[:].rearrange("p j (c i) -> p c j i", i=4)
-        weave = lambda ap: ap.rearrange("p (c i) j -> p c j i", i=4)
-        flat = lambda ap: ap.rearrange("p t j -> p (t j)")
-        nc.scalar.activation(weave(q[:, 0]), hv, ACT.Relu)
-        nc.scalar.activation(weave(qm[:]), hv, ACT.Relu, scale=-1.0)
-        nc.scalar.activation(flat(q[:, 1]), flat(qm[:]), ACT.Copy, scale=-1.0)
-        nc.vector.quantize_mx(out=q_c[:, 0].bitcast(FP8X4), scales=q_s[:, 0], in_=flat(q[:, 0]))
-        xw_g = keep.tile([P, S], U32, name="xw_g", align_bytes=64)
-        nc.vector.tensor_copy(xw_g[:], xw[:].bitcast(U32).indirect(offsets[:]))
-        qm_c = keep.tile([P, V], U32, name="qm_c", tag="xw", align_bytes=64)
-        nc.vector.quantize_mx(out=qm_c[:].bitcast(FP8X4), scales=q_s[:, 1], in_=flat(q[:, 1]))
-        ew_h = [keep.tile([P, S // 2], U32, name=f"ew_h{u}", align_bytes=64) for u in range(2)]
-        for u in range(2):
-            nc.vector.tensor_copy(ew_h[u][:], ew[:].bitcast(U32).indirect(offsets[:, 16 * u : 16 * u + 16]))
+        nc.vector.tensor_copy(e_scale_picked[:], e_scale_table[:].indirect(offsets[:]))
+        nc.vector.tensor_copy(x_scale_picked[:], x_scale_table[:].indirect(offsets[:]))
+        for r in range(PACK):
+            nc.sync.dma_start(out=e_scale_placed[E_ROW + r : P : GROUP, :].bitcast(I32),
+                              in_=e_scale_picked[STAGE + r : P : PACK, :].bitcast(I32))
 
-        H = S // 2
-        acc = [[psum.tile([P, H], F32, name=f"acc{b}{u}") for u in range(2)] for b in range(2)]
+        h_walk = h[:].rearrange("p j (c i) -> p c j i", i=PACK)
+        nc.scalar.activation(woven(qp[:]), h_walk, ACT.Relu)
+        nc.scalar.activation(woven(qm[:]), h_walk, ACT.Relu, scale=-1.0)
+        nc.scalar.activation(flat(qm_negated[:]), flat(qm[:]), ACT.Copy, scale=-1.0)
+        nc.vector.quantize_mx(out=qp_codes[:].bitcast(FP8X4), scales=qp_scales[:], in_=flat(qp[:]))
+
+        x_word_picked = keep.tile([P, S], U32, name="x_word_picked", align_bytes=64)
+        nc.vector.tensor_copy(x_word_picked[:], x_word_table[:].bitcast(U32).indirect(offsets[:]))
+        qm_codes = keep.tile([P, V], U32, name="qm_codes", tag="x_words_then_qm_codes", align_bytes=64)
+        nc.vector.quantize_mx(out=qm_codes[:].bitcast(FP8X4), scales=qm_scales[:], in_=flat(qm_negated[:]))
+        e_word_picked = [keep.tile([P, HALF], U32, name=f"e_word_picked{u}", align_bytes=64) for u in range(2)]
         for u in range(2):
-            n = slice(u * H, (u + 1) * H)
-            for b in range(2):
-                c = slice(b * P, (b + 1) * P)
-                nc.tensor.matmul_mx(out=acc[b][u][:], lhsT=q_c[:, 0, c].bitcast(FP8X4), lhsT_scale=q_s[:, 0, c],
-                                    rhs=xw_g[:, n].bitcast(FP8X4), rhs_scale=xs_g[:, n], start=True, stop=False)
-        for u in range(2):
-            n = slice(u * H, (u + 1) * H)
-            for b in range(2):
-                c = slice(b * P, (b + 1) * P)
-                nc.tensor.matmul_mx(out=acc[b][u][:], lhsT=qm_c[:, c].bitcast(FP8X4), lhsT_scale=q_s[:, 1, c],
-                                    rhs=ew_h[u][:].bitcast(FP8X4), rhs_scale=es_m[4:P, n], start=False, stop=True)
-        col = lambda name: keep.tile([P, 1], F32, name=name)
-        neg = [keep.tile([P, S], F32, name=f"neg{b}") for b in range(2)]
-        ex = [keep.tile([P, S], F32, name=f"ex{b}") for b in range(2)]
-        low0, low, inv = ([col(f"{name}{b}") for b in range(2)] for name in ("low0", "low", "inv"))
-        for b in range(2):
-            nc.vector.tensor_scalar(neg[b][:, :H], acc[b][0][:], -1.0, None, ALU.mult, ALU.min, accum_out=low0[b][:])
-            nc.vector.tensor_scalar(neg[b][:, H:], acc[b][1][:], -1.0, low0[b][:], ALU.mult, ALU.min, accum_out=low[b][:])
-        res = [[keep.tile([P, H], F32, name=f"res{b}{u}") for u in range(2)] for b in range(2)]
-        early, late, shift, tot0, tot1 = (col(name) for name in ("early", "late", "shift", "tot0", "tot1"))
-        nc.scalar.activation(ex[0][:, :H], neg[0][:, :H], ACT.Exp, bias=low0[0][:], scale=-1.0, accum_out=early[:])
-        nc.scalar.activation(shift[:], low0[0][:], ACT.Exp, bias=low[0][:], scale=-1.0)
-        nc.scalar.activation(ex[0][:, H:], neg[0][:, H:], ACT.Exp, bias=low[0][:], scale=-1.0, accum_out=late[:])
-        nc.vector.tensor_scalar(tot0[:], early[:], shift[:], late[:], ALU.mult, ALU.add)
-        nc.vector.reciprocal(inv[0][:], tot0[:])
-        nc.vector.tensor_scalar(res[0][0][:], ex[0][:, :H], shift[:], inv[0][:], ALU.mult, ALU.mult)
-        nc.sync.dma_start(out=out[:P, :H], in_=res[0][0][:])
-        nc.vector.tensor_scalar(res[0][1][:], ex[0][:, H:], inv[0][:], None, ALU.mult)
-        nc.sync.dma_start(out=out[:P, H:], in_=res[0][1][:])
-        nc.scalar.activation(ex[1][:], neg[1][:], ACT.Exp, bias=low[1][:], scale=-1.0, accum_out=tot1[:])
-        nc.vector.reciprocal(inv[1][:], tot1[:])
-        nc.vector.tensor_scalar(res[1][0][:], ex[1][:, :H], inv[1][:], None, ALU.mult)
-        nc.sync.dma_start(out=out[P:, :H], in_=res[1][0][:])
-        nc.scalar.activation(res[1][1][:], ex[1][:, H:], ACT.Copy, scale=inv[1][:])
-        nc.sync.dma_start(out=out[P:, H:], in_=res[1][1][:])
+            nc.vector.tensor_copy(e_word_picked[u][:], e_word_table[:].bitcast(U32).indirect(offsets[:, 16 * u : 16 * u + 16]))
+
+        y = [[psum.tile([P, HALF], F32, name=f"y{b}{u}") for u in range(2)] for b in range(2)]
+        for u, pages in enumerate(halves):
+            for b, cols in enumerate(queries):
+                nc.tensor.matmul_mx(out=y[b][u][:], lhsT=qp_codes[:, cols].bitcast(FP8X4), lhsT_scale=qp_scales[:, cols],
+                                    rhs=x_word_picked[:, pages].bitcast(FP8X4), rhs_scale=x_scale_picked[:, pages],
+                                    start=True, stop=False)
+        for u, pages in enumerate(halves):
+            for b, cols in enumerate(queries):
+                nc.tensor.matmul_mx(out=y[b][u][:], lhsT=qm_codes[:, cols].bitcast(FP8X4), lhsT_scale=qm_scales[:, cols],
+                                    rhs=e_word_picked[u][:].bitcast(FP8X4), rhs_scale=e_scale_placed[E_ROW:P, pages],
+                                    start=False, stop=True)
+
+        for b, rows in enumerate(queries):
+            half_min = keep.tile([P, 1], F32, name=f"half_min{b}")
+            row_min = keep.tile([P, 1], F32, name=f"row_min{b}")
+            total = keep.tile([P, 1], F32, name=f"total{b}")
+            inverse = keep.tile([P, 1], F32, name=f"inverse{b}")
+            minus_y = keep.tile([P, S], F32, name=f"minus_y{b}")
+            exps = keep.tile([P, S], F32, name=f"exps{b}")
+            nc.vector.tensor_scalar(minus_y[:, halves[0]], y[b][0][:], -1.0, None, ALU.mult, ALU.min, accum_out=half_min[:])
+            nc.vector.tensor_scalar(minus_y[:, halves[1]], y[b][1][:], -1.0, half_min[:], ALU.mult, ALU.min, accum_out=row_min[:])
+            nc.scalar.activation(exps[:], minus_y[:], ACT.Exp, bias=row_min[:], scale=-1.0, accum_out=total[:])
+            nc.vector.reciprocal(inverse[:], total[:])
+            for u, pages in enumerate(halves):
+                result = keep.tile([P, HALF], F32, name=f"result{b}{u}")
+                nc.vector.tensor_scalar(result[:], exps[:, pages], inverse[:], None, ALU.mult)
+                nc.sync.dma_start(out=out[rows, pages], in_=result[:])

@@ -20,6 +20,7 @@ PACK = 4
 GROUP = 32
 BLOCKS = K // 32
 HALF = S // 2
+QUARTER = S // 4
 E_ROW = 4
 STAGE = P - BLOCKS
 
@@ -87,28 +88,32 @@ def tile_picked_yquest_soft_p_kernel(tc, x_words, x_scales, e_words, e_scales, h
         for u in range(2):
             nc.vector.tensor_copy(e_word_picked[u][:], e_word_table[:].bitcast(U32).indirect(offsets[:, 16 * u : 16 * u + 16]))
 
-        y = [[psum.tile([P, HALF], F32, name=f"y{b}{u}") for u in range(2)] for b in range(2)]
-        for u, pages in enumerate(halves):
-            for b, cols in enumerate(queries):
-                nc.tensor.matmul_mx(out=y[b][u][:], lhsT=qp_codes[:, cols].bitcast(FP8X4), lhsT_scale=qp_scales[:, cols],
-                                    rhs=x_word_picked[:, pages].bitcast(FP8X4), rhs_scale=x_scale_picked[:, pages],
-                                    start=True, stop=False)
-        for u, pages in enumerate(halves):
-            for b, cols in enumerate(queries):
-                nc.tensor.matmul_mx(out=y[b][u][:], lhsT=qm_codes[:, cols].bitcast(FP8X4), lhsT_scale=qm_scales[:, cols],
-                                    rhs=e_word_picked[u][:].bitcast(FP8X4), rhs_scale=e_scale_placed[E_ROW:P, pages],
-                                    start=False, stop=True)
+        pieces = [(0, 0, HALF), (1, 0, QUARTER), (0, HALF, S), (1, QUARTER, S)]
+        y = [psum.tile([P, hi - lo], F32, name=f"y{n}") for n, (b, lo, hi) in enumerate(pieces)]
+        passes = [(0, 0, HALF), (1, 0, QUARTER), (3, QUARTER, HALF), (2, HALF, S), (3, HALF, S)]
+        for n, lo, hi in passes:
+            b, first, last = pieces[n]
+            nc.tensor.matmul_mx(out=y[n][:, lo - first : hi - first], lhsT=qp_codes[:, queries[b]].bitcast(FP8X4),
+                                lhsT_scale=qp_scales[:, queries[b]], rhs=x_word_picked[:, lo:hi].bitcast(FP8X4),
+                                rhs_scale=x_scale_picked[:, lo:hi], start=lo == first, stop=False)
+        for n, lo, hi in passes:
+            b, first, last = pieces[n]
+            u = lo // HALF
+            nc.tensor.matmul_mx(out=y[n][:, lo - first : hi - first], lhsT=qm_codes[:, queries[b]].bitcast(FP8X4),
+                                lhsT_scale=qm_scales[:, queries[b]],
+                                rhs=e_word_picked[u][:, lo - u * HALF : hi - u * HALF].bitcast(FP8X4),
+                                rhs_scale=e_scale_placed[E_ROW:P, lo:hi], start=False, stop=hi == last)
 
+        minus_y = [keep.tile([P, S], F32, name=f"minus_y{b}") for b in range(2)]
+        minimum = [keep.tile([P, 1], F32, name=f"minimum{n}") for n in range(4)]
+        for n, (b, lo, hi) in enumerate(pieces):
+            nc.vector.tensor_scalar(minus_y[b][:, lo:hi], y[n][:], -1.0, minimum[n - 2][:] if lo else None,
+                                    ALU.mult, ALU.min, accum_out=minimum[n][:])
         for b, rows in enumerate(queries):
-            half_min = keep.tile([P, 1], F32, name=f"half_min{b}")
-            row_min = keep.tile([P, 1], F32, name=f"row_min{b}")
             total = keep.tile([P, 1], F32, name=f"total{b}")
             inverse = keep.tile([P, 1], F32, name=f"inverse{b}")
-            minus_y = keep.tile([P, S], F32, name=f"minus_y{b}")
             exps = keep.tile([P, S], F32, name=f"exps{b}")
-            nc.vector.tensor_scalar(minus_y[:, halves[0]], y[b][0][:], -1.0, None, ALU.mult, ALU.min, accum_out=half_min[:])
-            nc.vector.tensor_scalar(minus_y[:, halves[1]], y[b][1][:], -1.0, half_min[:], ALU.mult, ALU.min, accum_out=row_min[:])
-            nc.scalar.activation(exps[:], minus_y[:], ACT.Exp, bias=row_min[:], scale=-1.0, accum_out=total[:])
+            nc.scalar.activation(exps[:], minus_y[b][:], ACT.Exp, bias=minimum[2 + b][:], scale=-1.0, accum_out=total[:])
             nc.vector.reciprocal(inverse[:], total[:])
             for u, pages in enumerate(halves):
                 result = keep.tile([P, HALF], F32, name=f"result{b}{u}")

@@ -71,8 +71,9 @@ def tile_picked_yquest_soft_p_kernel(tc, x_words, x_scales, e_words, e_scales, h
         nc.vector.tensor_copy(e_scale_picked[:], e_scale_table[:].indirect(offsets[:]))
         nc.vector.tensor_copy(x_scale_picked[:], x_scale_table[:].indirect(offsets[:]))
         for r in range(PACK):
-            nc.sync.dma_start(out=e_scale_placed[E_ROW + r : P : GROUP, :].bitcast(I32),
-                              in_=e_scale_picked[STAGE + r : P : PACK, :].bitcast(I32))
+            queue = nc.sync if r else nc.gpsimd
+            queue.dma_start(out=e_scale_placed[E_ROW + r : P : GROUP, :].bitcast(I32),
+                            in_=e_scale_picked[STAGE + r : P : PACK, :].bitcast(I32))
 
         h_walk = h[:].rearrange("p j (c i) -> p c j i", i=PACK)
         nc.scalar.activation(woven(qp[:]), h_walk, ACT.Relu)
@@ -80,8 +81,9 @@ def tile_picked_yquest_soft_p_kernel(tc, x_words, x_scales, e_words, e_scales, h
         nc.scalar.activation(flat(qm_negated[:]), flat(qm[:]), ACT.Copy, scale=-1.0)
         nc.vector.quantize_mx(out=qp_codes[:].bitcast(FP8X4), scales=qp_scales[:], in_=flat(qp[:]))
 
-        x_word_picked = keep.tile([P, S], U32, name="x_word_picked", align_bytes=64)
-        nc.vector.tensor_copy(x_word_picked[:], x_word_table[:].bitcast(U32).indirect(offsets[:]))
+        x_word_picked = [keep.tile([P, HALF], U32, name=f"x_word_picked{u}", align_bytes=64) for u in range(2)]
+        for u in range(2):
+            nc.vector.tensor_copy(x_word_picked[u][:], x_word_table[:].bitcast(U32).indirect(offsets[:, 16 * u : 16 * u + 16]))
         qm_codes = keep.tile([P, V], U32, name="qm_codes", tag="x_words_then_qm_codes", align_bytes=64)
         nc.vector.quantize_mx(out=qm_codes[:].bitcast(FP8X4), scales=qm_scales[:], in_=flat(qm_negated[:]))
         e_word_picked = [keep.tile([P, HALF], U32, name=f"e_word_picked{u}", align_bytes=64) for u in range(2)]
@@ -93,8 +95,10 @@ def tile_picked_yquest_soft_p_kernel(tc, x_words, x_scales, e_words, e_scales, h
         passes = [(0, 0, HALF), (1, 0, QUARTER), (3, QUARTER, HALF), (2, HALF, S), (3, HALF, S)]
         for n, lo, hi in passes:
             b, first, last = pieces[n]
+            u = lo // HALF
             nc.tensor.matmul_mx(out=y[n][:, lo - first : hi - first], lhsT=qp_codes[:, queries[b]].bitcast(FP8X4),
-                                lhsT_scale=qp_scales[:, queries[b]], rhs=x_word_picked[:, lo:hi].bitcast(FP8X4),
+                                lhsT_scale=qp_scales[:, queries[b]],
+                                rhs=x_word_picked[u][:, lo - u * HALF : hi - u * HALF].bitcast(FP8X4),
                                 rhs_scale=x_scale_picked[:, lo:hi], start=lo == first, stop=False)
         for n, lo, hi in passes:
             b, first, last = pieces[n]

@@ -22,7 +22,7 @@ BLOCKS = K // 32
 HALF = S // 2
 QUARTER = S // 4
 E_ROW = 4
-STAGE = P - BLOCKS
+STAGE = 32
 
 
 def tile_picked_yquest_soft_p_kernel(tc, x_words, x_scales, e_words, e_scales, hT, offs, out):
@@ -56,13 +56,13 @@ def tile_picked_yquest_soft_p_kernel(tc, x_words, x_scales, e_words, e_scales, h
         qp_scales = keep.tile([P, V], U8, name="qp_scales", align_bytes=64)
         qm_scales = keep.tile([P, V], U8, name="qm_scales", align_bytes=64)
 
+        nc.vector.memset(e_scale_table[:].bitcast(I32), 0)
         nc.vector.memset(x_scale_table[:].bitcast(I32), 0)
-        nc.vector.memset(e_scale_table[:STAGE, :].bitcast(I32), 0)
         nc.vector.memset(e_scale_placed[:].bitcast(I32), 0)
 
         nc.sync.dma_start(out=h[:], in_=hT.rearrange("(p j) t -> p j t", j=PACK))
         nc.sync.dma_start(offsets[:], offs)
-        nc.sync.dma_start(out=e_scale_table[STAGE:, :].bitcast(I32), in_=e_scales[0].bitcast(I32))
+        nc.sync.dma_start(out=e_scale_table[STAGE : STAGE + PACK * BLOCKS : PACK, :].bitcast(I32), in_=e_scales[0].bitcast(I32))
         for r in range(PACK):
             nc.sync.dma_start(out=x_scale_table[r:P:GROUP, :].bitcast(I32), in_=x_scales[0, r:BLOCKS:PACK, :].bitcast(I32))
         nc.sync.dma_start(out=x_word_table[:], in_=x_words[0].rearrange("p n t -> p (n t)").bitcast(I32))
@@ -73,7 +73,7 @@ def tile_picked_yquest_soft_p_kernel(tc, x_words, x_scales, e_words, e_scales, h
         for r in range(PACK):
             queue = nc.sync if r else nc.gpsimd
             queue.dma_start(out=e_scale_placed[E_ROW + r : P : GROUP, :].bitcast(I32),
-                            in_=e_scale_picked[STAGE + r : P : PACK, :].bitcast(I32))
+                            in_=e_scale_picked[STAGE + PACK * r : STAGE + PACK * BLOCKS : PACK * PACK, :].bitcast(I32))
 
         h_walk = h[:].rearrange("p j (c i) -> p c j i", i=PACK)
         nc.scalar.activation(woven(qp[:]), h_walk, ACT.Relu)

@@ -22,6 +22,7 @@ BLOCKS = K // 32
 HALF = S // 2
 QUARTER = S // 4
 E_ROW = 4
+X_STAGE = P - BLOCKS
 STAGE = 32
 
 
@@ -41,13 +42,13 @@ def tile_picked_yquest_soft_p_kernel(tc, x_words, x_scales, e_words, e_scales, h
         psum = ctx.enter_context(tc.psum_pool(name="psum", bufs=1))
 
         offsets = keep.tile([P, S // 16], U16, name="offsets")
-        x_scale_table = keep.tile([P, T], U8, name="x_scale_table", align_bytes=64)
+        x_scale_table = keep.tile([P, T], U8, name="x_scale_table", tag="x_scales_then_e_words", align_bytes=64)
         e_scale_table = keep.tile([P, T], U8, name="e_scale_table", align_bytes=64)
         x_word_table = keep.tile([P, T], I32, name="x_word_table", tag="x_words_then_qm_codes", align_bytes=64)
-        e_word_table = keep.tile([P, T], I32, name="e_word_table", align_bytes=64)
         h = keep.tile([P, PACK, V], F32, name="h", align_bytes=64)
         x_scale_picked = keep.tile([P, S], U8, name="x_scale_picked", align_bytes=64)
         e_scale_picked = keep.tile([P, S], U8, name="e_scale_picked", align_bytes=64)
+        x_scale_placed = keep.tile([P, S], U8, name="x_scale_placed", align_bytes=64)
         e_scale_placed = keep.tile([P, S], U8, name="e_scale_placed", align_bytes=64)
         qp = keep.tile([P, V, PACK], BF16, name="qp", align_bytes=64)
         qm = keep.tile([P, V, PACK], BF16, name="qm", align_bytes=64)
@@ -56,22 +57,27 @@ def tile_picked_yquest_soft_p_kernel(tc, x_words, x_scales, e_words, e_scales, h
         qp_scales = keep.tile([P, V], U8, name="qp_scales", align_bytes=64)
         qm_scales = keep.tile([P, V], U8, name="qm_scales", align_bytes=64)
 
+        nc.vector.memset(x_scale_table[0:X_STAGE, :].bitcast(I32), 0)
         nc.vector.memset(e_scale_table[:].bitcast(I32), 0)
-        nc.vector.memset(x_scale_table[:].bitcast(I32), 0)
+        nc.vector.memset(x_scale_placed[:].bitcast(I32), 0)
         nc.vector.memset(e_scale_placed[:].bitcast(I32), 0)
 
-        nc.sync.dma_start(out=h[:], in_=hT.rearrange("(p j) t -> p j t", j=PACK))
         nc.sync.dma_start(offsets[:], offs)
+        nc.scalar.dma_start(out=x_scale_table[X_STAGE:P, :].bitcast(I32), in_=x_scales[0].bitcast(I32))
+        nc.sync.dma_start(out=h[:], in_=hT.rearrange("(p j) t -> p j t", j=PACK))
         nc.sync.dma_start(out=e_scale_table[STAGE : STAGE + PACK * BLOCKS : PACK, :].bitcast(I32), in_=e_scales[0].bitcast(I32))
-        for r in range(PACK):
-            nc.sync.dma_start(out=x_scale_table[r:P:GROUP, :].bitcast(I32), in_=x_scales[0, r:BLOCKS:PACK, :].bitcast(I32))
         nc.sync.dma_start(out=x_word_table[:], in_=x_words[0].rearrange("p n t -> p (n t)").bitcast(I32))
+
+        nc.vector.tensor_copy(x_scale_picked[:], x_scale_table[:].indirect(offsets[:]))
+        for r in range(PACK):
+            nc.sync.dma_start(out=x_scale_placed[r:P:GROUP, :].bitcast(I32),
+                              in_=x_scale_picked[X_STAGE + r : P : PACK, :].bitcast(I32))
+        e_word_table = keep.tile([P, T], I32, name="e_word_table", tag="x_scales_then_e_words", align_bytes=64)
         nc.sync.dma_start(out=e_word_table[:], in_=e_words[0].rearrange("p n t -> p (n t)").bitcast(I32))
 
         nc.vector.tensor_copy(e_scale_picked[:], e_scale_table[:].indirect(offsets[:]))
-        nc.vector.tensor_copy(x_scale_picked[:], x_scale_table[:].indirect(offsets[:]))
         for r in range(PACK):
-            queue = nc.sync if r else nc.gpsimd
+            queue = nc.sync if r > 1 else nc.gpsimd
             queue.dma_start(out=e_scale_placed[E_ROW + r : P : GROUP, :].bitcast(I32),
                             in_=e_scale_picked[STAGE + PACK * r : STAGE + PACK * BLOCKS : PACK * PACK, :].bitcast(I32))
 
@@ -99,7 +105,7 @@ def tile_picked_yquest_soft_p_kernel(tc, x_words, x_scales, e_words, e_scales, h
             nc.tensor.matmul_mx(out=y[n][:, lo - first : hi - first], lhsT=qp_codes[:, queries[b]].bitcast(FP8X4),
                                 lhsT_scale=qp_scales[:, queries[b]],
                                 rhs=x_word_picked[u][:, lo - u * HALF : hi - u * HALF].bitcast(FP8X4),
-                                rhs_scale=x_scale_picked[:, lo:hi], start=lo == first, stop=False)
+                                rhs_scale=x_scale_placed[:, lo:hi], start=lo == first, stop=False)
         for n, lo, hi in passes:
             b, first, last = pieces[n]
             u = lo // HALF

@@ -23,7 +23,7 @@ HALF = S // 2
 QUARTER = S // 4
 E_ROW = 4
 X_STAGE = P - BLOCKS
-STAGE = 32
+E_STEP = P // BLOCKS
 
 
 def tile_picked_yquest_soft_p_kernel(tc, x_words, x_scales, e_words, e_scales, hT, offs, out):
@@ -60,26 +60,26 @@ def tile_picked_yquest_soft_p_kernel(tc, x_words, x_scales, e_words, e_scales, h
         nc.vector.memset(x_scale_table[0:X_STAGE, :].bitcast(I32), 0)
         nc.vector.memset(e_scale_table[:].bitcast(I32), 0)
         nc.vector.memset(x_scale_placed[:].bitcast(I32), 0)
-        nc.vector.memset(e_scale_placed[:].bitcast(I32), 0)
 
         nc.sync.dma_start(offsets[:], offs)
         nc.scalar.dma_start(out=x_scale_table[X_STAGE:P, :].bitcast(I32), in_=x_scales[0].bitcast(I32))
         nc.sync.dma_start(out=h[:], in_=hT.rearrange("(p j) t -> p j t", j=PACK))
-        nc.sync.dma_start(out=e_scale_table[STAGE : STAGE + PACK * BLOCKS : PACK, :].bitcast(I32), in_=e_scales[0].bitcast(I32))
+        nc.sync.dma_start(out=e_scale_table[E_ROW:P:E_STEP, :].bitcast(I32), in_=e_scales[0].bitcast(I32))
         nc.sync.dma_start(out=x_word_table[:], in_=x_words[0].rearrange("p n t -> p (n t)").bitcast(I32))
 
         nc.vector.tensor_copy(x_scale_picked[:], x_scale_table[:].indirect(offsets[:]))
         for r in range(PACK):
-            nc.sync.dma_start(out=x_scale_placed[r:P:GROUP, :].bitcast(I32),
-                              in_=x_scale_picked[X_STAGE + r : P : PACK, :].bitcast(I32))
+            queue = nc.sync if r else nc.gpsimd
+            queue.dma_start(out=x_scale_placed[r:P:GROUP, :].bitcast(I32),
+                            in_=x_scale_picked[X_STAGE + r : P : PACK, :].bitcast(I32))
         e_word_table = keep.tile([P, T], I32, name="e_word_table", tag="x_scales_then_e_words", align_bytes=64)
         nc.sync.dma_start(out=e_word_table[:], in_=e_words[0].rearrange("p n t -> p (n t)").bitcast(I32))
 
         nc.vector.tensor_copy(e_scale_picked[:], e_scale_table[:].indirect(offsets[:]))
-        for r in range(PACK):
-            queue = nc.sync if r > 1 else nc.gpsimd
-            queue.dma_start(out=e_scale_placed[E_ROW + r : P : GROUP, :].bitcast(I32),
-                            in_=e_scale_picked[STAGE + PACK * r : STAGE + PACK * BLOCKS : PACK * PACK, :].bitcast(I32))
+        nc.vector.tensor_copy(e_scale_placed[:].bitcast(I32), e_scale_picked[:].bitcast(I32))
+        for r in range(1, PACK):
+            nc.sync.dma_start(out=e_scale_placed[E_ROW + r : P : GROUP, :].bitcast(I32),
+                              in_=e_scale_picked[E_ROW + E_STEP * r : P : GROUP, :].bitcast(I32))
 
         h_walk = h[:].rearrange("p j (c i) -> p c j i", i=PACK)
         nc.scalar.activation(woven(qp[:]), h_walk, ACT.Relu)

@@ -69,17 +69,17 @@ def tile_picked_yquest_soft_p_kernel(tc, x_words, x_scales, e_words, e_scales, h
 
         nc.vector.tensor_copy(x_scale_picked[:], x_scale_table[:].indirect(offsets[:]))
         for r in range(PACK):
-            queue = nc.sync if r else nc.gpsimd
-            queue.dma_start(out=x_scale_placed[r:P:GROUP, :].bitcast(I32),
-                            in_=x_scale_picked[X_STAGE + r : P : PACK, :].bitcast(I32))
+            nc.sync.dma_start(out=x_scale_placed[r:P:GROUP, :].bitcast(I32),
+                              in_=x_scale_picked[X_STAGE + r : P : PACK, :].bitcast(I32))
         e_word_table = keep.tile([P, T], I32, name="e_word_table", tag="x_scales_then_e_words", align_bytes=64)
         nc.sync.dma_start(out=e_word_table[:], in_=e_words[0].rearrange("p n t -> p (n t)").bitcast(I32))
 
         nc.vector.tensor_copy(e_scale_picked[:], e_scale_table[:].indirect(offsets[:]))
         nc.vector.tensor_copy(e_scale_placed[:].bitcast(I32), e_scale_picked[:].bitcast(I32))
         for r in range(1, PACK):
-            nc.sync.dma_start(out=e_scale_placed[E_ROW + r : P : GROUP, :].bitcast(I32),
-                              in_=e_scale_picked[E_ROW + E_STEP * r : P : GROUP, :].bitcast(I32))
+            queue = nc.sync if r > 1 else nc.gpsimd
+            queue.dma_start(out=e_scale_placed[E_ROW + r : P : GROUP, :].bitcast(I32),
+                            in_=e_scale_picked[E_ROW + E_STEP * r : P : GROUP, :].bitcast(I32))
 
         h_walk = h[:].rearrange("p j (c i) -> p c j i", i=PACK)
         nc.scalar.activation(woven(qp[:]), h_walk, ACT.Relu)

@@ -43,7 +43,7 @@ def tile_picked_yquest_soft_p_kernel(tc, x_words, x_scales, e_words, e_scales, h
 
         offsets = keep.tile([P, S // 16], U16, name="offsets")
         x_scale_table = keep.tile([P, T], U8, name="x_scale_table", tag="x_scales_then_e_words", align_bytes=64)
-        e_scale_table = keep.tile([P, T], U8, name="e_scale_table", align_bytes=64)
+        e_scale_table = keep.tile([P, T], U8, name="e_scale_table", tag="e_scales_then_qm", align_bytes=64)
         x_word_table = keep.tile([P, T], I32, name="x_word_table", tag="x_words_then_qm_codes", align_bytes=64)
         h = keep.tile([P, PACK, V], F32, name="h", align_bytes=64)
         x_scale_picked = keep.tile([P, S], U8, name="x_scale_picked", align_bytes=64)
@@ -51,8 +51,6 @@ def tile_picked_yquest_soft_p_kernel(tc, x_words, x_scales, e_words, e_scales, h
         x_scale_placed = keep.tile([P, S], U8, name="x_scale_placed", align_bytes=64)
         e_scale_placed = keep.tile([P, S], U8, name="e_scale_placed", align_bytes=64)
         qp = keep.tile([P, V, PACK], BF16, name="qp", align_bytes=64)
-        qm = keep.tile([P, V, PACK], BF16, name="qm", align_bytes=64)
-        qm_negated = keep.tile([P, V, PACK], BF16, name="qm_negated", align_bytes=64)
         qp_codes = keep.tile([P, V], U32, name="qp_codes", align_bytes=64)
         qp_scales = keep.tile([P, V], U8, name="qp_scales", align_bytes=64)
         qm_scales = keep.tile([P, V], U8, name="qm_scales", align_bytes=64)
@@ -60,6 +58,10 @@ def tile_picked_yquest_soft_p_kernel(tc, x_words, x_scales, e_words, e_scales, h
         nc.vector.memset(x_scale_table[0:X_STAGE, :].bitcast(I32), 0)
         nc.vector.memset(e_scale_table[:].bitcast(I32), 0)
         nc.vector.memset(x_scale_placed[:].bitcast(I32), 0)
+
+        table_load = keep.tile([P, 1], F32, name="table_load")
+        nc.vector.memset(table_load[:], 0.0)
+        nc.scalar.activation(table_load[:], table_load[:], ACT.Exp)
 
         nc.sync.dma_start(offsets[:], offs)
         nc.scalar.dma_start(out=x_scale_table[X_STAGE:P, :].bitcast(I32), in_=x_scales[0].bitcast(I32))
@@ -69,8 +71,9 @@ def tile_picked_yquest_soft_p_kernel(tc, x_words, x_scales, e_words, e_scales, h
 
         nc.vector.tensor_copy(x_scale_picked[:], x_scale_table[:].indirect(offsets[:]))
         for r in range(PACK):
-            nc.sync.dma_start(out=x_scale_placed[r:P:GROUP, :].bitcast(I32),
-                              in_=x_scale_picked[X_STAGE + r : P : PACK, :].bitcast(I32))
+            queue = nc.sync if r % 2 else nc.scalar
+            queue.dma_start(out=x_scale_placed[r:P:GROUP, :].bitcast(I32),
+                            in_=x_scale_picked[X_STAGE + r : P : PACK, :].bitcast(I32))
         e_word_table = keep.tile([P, T], I32, name="e_word_table", tag="x_scales_then_e_words", align_bytes=64)
         nc.sync.dma_start(out=e_word_table[:], in_=e_words[0].rearrange("p n t -> p (n t)").bitcast(I32))
 
@@ -83,8 +86,8 @@ def tile_picked_yquest_soft_p_kernel(tc, x_words, x_scales, e_words, e_scales, h
 
         h_walk = h[:].rearrange("p j (c i) -> p c j i", i=PACK)
         nc.scalar.activation(woven(qp[:]), h_walk, ACT.Relu)
-        nc.scalar.activation(woven(qm[:]), h_walk, ACT.Relu, scale=-1.0)
-        nc.scalar.activation(flat(qm_negated[:]), flat(qm[:]), ACT.Copy, scale=-1.0)
+        qm_negated = keep.tile([P, V, PACK], BF16, name="qm_negated", tag="e_scales_then_qm", align_bytes=64)
+        nc.vector.tensor_scalar(woven(qm_negated[:]), h_walk, 0.0, None, ALU.min)
         nc.vector.quantize_mx(out=qp_codes[:].bitcast(FP8X4), scales=qp_scales[:], in_=flat(qp[:]))
 
         x_word_picked = [keep.tile([P, HALF], U32, name=f"x_word_picked{u}", align_bytes=64) for u in range(2)]

@@ -96,8 +96,10 @@ def tile_picked_yquest_soft_p_kernel(tc, x_words, x_scales, e_words, e_scales, h
         qm_codes = keep.tile([P, V], U32, name="qm_codes", tag="x_words_then_qm_codes", align_bytes=64)
         nc.vector.quantize_mx(out=qm_codes[:].bitcast(FP8X4), scales=qm_scales[:], in_=flat(qm_negated[:]))
         e_word_picked = [keep.tile([P, HALF], U32, name=f"e_word_picked{u}", align_bytes=64) for u in range(2)]
-        for u in range(2):
-            nc.vector.tensor_copy(e_word_picked[u][:], e_word_table[:].bitcast(U32).indirect(offsets[:, 16 * u : 16 * u + 16]))
+        for lo, hi in [(0, HALF), (HALF, HALF + QUARTER), (HALF + QUARTER, S)]:
+            u = lo // HALF
+            nc.vector.tensor_copy(e_word_picked[u][:, lo - u * HALF : hi - u * HALF],
+                                  e_word_table[:].bitcast(U32).indirect(offsets[:, lo // 16 : hi // 16]))
 
         pieces = [(0, 0, HALF), (1, 0, QUARTER), (0, HALF, S), (1, QUARTER, S)]
         y = [psum.tile([P, hi - lo], F32, name=f"y{n}") for n, (b, lo, hi) in enumerate(pieces)]
@@ -109,7 +111,8 @@ def tile_picked_yquest_soft_p_kernel(tc, x_words, x_scales, e_words, e_scales, h
                                 lhsT_scale=qp_scales[:, queries[b]],
                                 rhs=x_word_picked[u][:, lo - u * HALF : hi - u * HALF].bitcast(FP8X4),
                                 rhs_scale=x_scale_placed[:, lo:hi], start=lo == first, stop=False)
-        for n, lo, hi in passes:
+        e_passes = [(0, 0, HALF), (1, 0, QUARTER), (2, HALF, HALF + QUARTER), (2, HALF + QUARTER, S), (3, QUARTER, HALF), (3, HALF, S)]
+        for n, lo, hi in e_passes:
             b, first, last = pieces[n]
             u = lo // HALF
             nc.tensor.matmul_mx(out=y[n][:, lo - first : hi - first], lhsT=qm_codes[:, queries[b]].bitcast(FP8X4),

@@ -96,14 +96,15 @@ def tile_picked_yquest_soft_p_kernel(tc, x_words, x_scales, e_words, e_scales, h
         qm_codes = keep.tile([P, V], U32, name="qm_codes", tag="x_words_then_qm_codes", align_bytes=64)
         nc.vector.quantize_mx(out=qm_codes[:].bitcast(FP8X4), scales=qm_scales[:], in_=flat(qm_negated[:]))
         e_word_picked = [keep.tile([P, HALF], U32, name=f"e_word_picked{u}", align_bytes=64) for u in range(2)]
-        for lo, hi in [(0, HALF), (HALF, HALF + QUARTER), (HALF + QUARTER, S)]:
+        for lo in range(0, S, QUARTER):
+            hi = lo + QUARTER
             u = lo // HALF
             nc.vector.tensor_copy(e_word_picked[u][:, lo - u * HALF : hi - u * HALF],
                                   e_word_table[:].bitcast(U32).indirect(offsets[:, lo // 16 : hi // 16]))
 
         pieces = [(0, 0, HALF), (1, 0, QUARTER), (0, HALF, S), (1, QUARTER, S)]
         y = [psum.tile([P, hi - lo], F32, name=f"y{n}") for n, (b, lo, hi) in enumerate(pieces)]
-        passes = [(0, 0, HALF), (1, 0, QUARTER), (3, QUARTER, HALF), (2, HALF, S), (3, HALF, S)]
+        passes = [(0, 0, HALF), (1, 0, QUARTER), (3, QUARTER, HALF), (3, HALF, S), (2, HALF, S)]
         for n, lo, hi in passes:
             b, first, last = pieces[n]
             u = lo // HALF
@@ -111,7 +112,8 @@ def tile_picked_yquest_soft_p_kernel(tc, x_words, x_scales, e_words, e_scales, h
                                 lhsT_scale=qp_scales[:, queries[b]],
                                 rhs=x_word_picked[u][:, lo - u * HALF : hi - u * HALF].bitcast(FP8X4),
                                 rhs_scale=x_scale_placed[:, lo:hi], start=lo == first, stop=False)
-        e_passes = [(0, 0, HALF), (1, 0, QUARTER), (2, HALF, HALF + QUARTER), (2, HALF + QUARTER, S), (3, QUARTER, HALF), (3, HALF, S)]
+        e_passes = [(0, 0, QUARTER), (0, QUARTER, HALF), (1, 0, QUARTER), (3, QUARTER, HALF),
+                    (2, HALF, HALF + QUARTER), (2, HALF + QUARTER, S), (3, HALF, S)]
         for n, lo, hi in e_passes:
             b, first, last = pieces[n]
             u = lo // HALF
@@ -131,7 +133,7 @@ def tile_picked_yquest_soft_p_kernel(tc, x_words, x_scales, e_words, e_scales, h
             exps = keep.tile([P, S], F32, name=f"exps{b}")
             nc.scalar.activation(exps[:], minus_y[b][:], ACT.Exp, bias=minimum[2 + b][:], scale=-1.0, accum_out=total[:])
             nc.vector.reciprocal(inverse[:], total[:])
-            for u, pages in enumerate(halves):
-                result = keep.tile([P, HALF], F32, name=f"result{b}{u}")
+            for u, pages in enumerate([slice(0, QUARTER), slice(QUARTER, S)]):
+                result = keep.tile([P, pages.stop - pages.start], F32, name=f"result{b}{u}")
                 nc.vector.tensor_scalar(result[:], exps[:, pages], inverse[:], None, ALU.mult)
                 nc.sync.dma_start(out=out[rows, pages], in_=result[:])

@@ -23,7 +23,6 @@ HALF = S // 2
 QUARTER = S // 4
 E_ROW = 4
 X_STAGE = P - BLOCKS
-E_STEP = P // BLOCKS
 
 
 def tile_picked_yquest_soft_p_kernel(tc, x_words, x_scales, e_words, e_scales, hT, offs, out):
@@ -58,6 +57,7 @@ def tile_picked_yquest_soft_p_kernel(tc, x_words, x_scales, e_words, e_scales, h
         nc.vector.memset(x_scale_table[0:X_STAGE, :].bitcast(I32), 0)
         nc.vector.memset(e_scale_table[:].bitcast(I32), 0)
         nc.vector.memset(x_scale_placed[:].bitcast(I32), 0)
+        nc.vector.memset(e_scale_placed[:].bitcast(I32), 0)
 
         table_load = keep.tile([P, 1], F32, name="table_load")
         nc.vector.memset(table_load[:], 0.0)
@@ -66,7 +66,7 @@ def tile_picked_yquest_soft_p_kernel(tc, x_words, x_scales, e_words, e_scales, h
         nc.sync.dma_start(offsets[:], offs)
         nc.scalar.dma_start(out=x_scale_table[X_STAGE:P, :].bitcast(I32), in_=x_scales[0].bitcast(I32))
         nc.sync.dma_start(out=h[:], in_=hT.rearrange("(p j) t -> p j t", j=PACK))
-        nc.sync.dma_start(out=e_scale_table[E_ROW:P:E_STEP, :].bitcast(I32), in_=e_scales[0].bitcast(I32))
+        nc.sync.dma_start(out=e_scale_table[0 : PACK * BLOCKS : PACK, :].bitcast(I32), in_=e_scales[0].bitcast(I32))
         nc.sync.dma_start(out=x_word_table[:], in_=x_words[0].rearrange("p n t -> p (n t)").bitcast(I32))
 
         nc.vector.tensor_copy(x_scale_picked[:], x_scale_table[:].indirect(offsets[:]))
@@ -78,11 +78,10 @@ def tile_picked_yquest_soft_p_kernel(tc, x_words, x_scales, e_words, e_scales, h
         nc.sync.dma_start(out=e_word_table[:], in_=e_words[0].rearrange("p n t -> p (n t)").bitcast(I32))
 
         nc.vector.tensor_copy(e_scale_picked[:], e_scale_table[:].indirect(offsets[:]))
-        nc.vector.tensor_copy(e_scale_placed[:].bitcast(I32), e_scale_picked[:].bitcast(I32))
-        for r in range(1, PACK):
+        for r in range(PACK):
             queue = nc.sync if r > 1 else nc.gpsimd
             queue.dma_start(out=e_scale_placed[E_ROW + r : P : GROUP, :].bitcast(I32),
-                            in_=e_scale_picked[E_ROW + E_STEP * r : P : GROUP, :].bitcast(I32))
+                            in_=e_scale_picked[PACK * r : PACK * BLOCKS : PACK * PACK, :].bitcast(I32))
 
         h_walk = h[:].rearrange("p j (c i) -> p c j i", i=PACK)
         nc.scalar.activation(woven(qp[:]), h_walk, ACT.Relu)

@@ -86,7 +86,11 @@ def tile_picked_yquest_soft_p_kernel(tc, x_words, x_scales, e_words, e_scales, h
         h_walk = h[:].rearrange("p j (c i) -> p c j i", i=PACK)
         nc.scalar.activation(woven(qp[:]), h_walk, ACT.Relu)
         qm_negated = keep.tile([P, V, PACK], BF16, name="qm_negated", tag="e_scales_then_qm", align_bytes=64)
-        nc.vector.tensor_scalar(woven(qm_negated[:]), h_walk, 0.0, None, ALU.min)
+        share = V // 2 // PACK
+        nc.vector.tensor_scalar(woven(qm_negated[:])[:, :share], h_walk[:, :share], 0.0, None, ALU.min)
+        qm_half = keep.tile([P, V // 2, PACK], BF16, name="qm_half", align_bytes=64)
+        nc.scalar.activation(woven(qm_half[:]), h_walk[:, share:], ACT.Relu, scale=-1.0)
+        nc.scalar.activation(flat(qm_negated[:, V // 2 :, :]), flat(qm_half[:]), ACT.Copy, scale=-1.0)
         nc.vector.quantize_mx(out=qp_codes[:].bitcast(FP8X4), scales=qp_scales[:], in_=flat(qp[:]))
 
         x_word_picked = [keep.tile([P, HALF], U32, name=f"x_word_picked{u}", align_bytes=64) for u in range(2)]

@@ -22,6 +22,7 @@ BLOCKS = K // 32
 HALF = S // 2
 QUARTER = S // 4
 E_ROW = 4
+E_STAGE = 32
 X_STAGE = P - BLOCKS
 
 
@@ -66,7 +67,7 @@ def tile_picked_yquest_soft_p_kernel(tc, x_words, x_scales, e_words, e_scales, h
         nc.sync.dma_start(offsets[:], offs)
         nc.scalar.dma_start(out=x_scale_table[X_STAGE:P, :].bitcast(I32), in_=x_scales[0].bitcast(I32))
         nc.sync.dma_start(out=h[:], in_=hT.rearrange("(p j) t -> p j t", j=PACK))
-        nc.sync.dma_start(out=e_scale_table[0 : PACK * BLOCKS : PACK, :].bitcast(I32), in_=e_scales[0].bitcast(I32))
+        nc.sync.dma_start(out=e_scale_table[E_STAGE : E_STAGE + PACK * BLOCKS : PACK, :].bitcast(I32), in_=e_scales[0].bitcast(I32))
         nc.sync.dma_start(out=x_word_table[:], in_=x_words[0].rearrange("p n t -> p (n t)").bitcast(I32))
 
         nc.vector.tensor_copy(x_scale_picked[:], x_scale_table[:].indirect(offsets[:]))
@@ -81,7 +82,7 @@ def tile_picked_yquest_soft_p_kernel(tc, x_words, x_scales, e_words, e_scales, h
         for r in range(PACK):
             queue = nc.sync if r > 1 else nc.gpsimd
             queue.dma_start(out=e_scale_placed[E_ROW + r : P : GROUP, :].bitcast(I32),
-                            in_=e_scale_picked[PACK * r : PACK * BLOCKS : PACK * PACK, :].bitcast(I32))
+                            in_=e_scale_picked[E_STAGE + PACK * r : E_STAGE + PACK * BLOCKS : PACK * PACK, :].bitcast(I32))
 
         h_walk = h[:].rearrange("p j (c i) -> p c j i", i=PACK)
         nc.scalar.activation(woven(qp[:]), h_walk, ACT.Relu)

from contextlib import ExitStack

import concourse.mybir as mybir

K, T, S, V = 512, 2048, 512, 256
FLOPS = 2 * 2 * K * V * S

F32 = mybir.dt.float32
BF16 = mybir.dt.bfloat16
I32 = mybir.dt.int32
U32 = mybir.dt.uint32
U16 = mybir.dt.uint16
U8 = mybir.dt.uint8
FP8X4 = mybir.dt.float8_e4m3fn_x4
ALU = mybir.AluOpType
ACT = mybir.ActivationFunctionType

P = 128
PACK = 4
GROUP = 32
BLOCKS = K // 32
HALF = S // 2
QUARTER = S // 4
E_ROW = 4
E_STAGE = 32
X_STAGE = P - BLOCKS


def tile_picked_yquest_soft_p_kernel(tc, x_words, x_scales, e_words, e_scales, hT, offs, out):
    nc = tc.nc
    halves = [slice(u * HALF, (u + 1) * HALF) for u in range(2)]
    queries = [slice(b * P, (b + 1) * P) for b in range(V // P)]

    def woven(ap):
        return ap.rearrange("p (c i) j -> p c j i", i=PACK)

    def flat(ap):
        return ap.rearrange("p t j -> p (t j)")

    with ExitStack() as ctx:
        keep = ctx.enter_context(tc.tile_pool(name="keep", bufs=1))
        psum = ctx.enter_context(tc.psum_pool(name="psum", bufs=1))

        offsets = keep.tile([P, S // 16], U16, name="offsets")
        x_scale_table = keep.tile([P, T], U8, name="x_scale_table", tag="x_scales_then_e_words", align_bytes=64)
        e_scale_table = keep.tile([P, T], U8, name="e_scale_table", tag="e_scales_then_qm", align_bytes=64)
        x_word_table = keep.tile([P, T], I32, name="x_word_table", tag="x_words_then_qm_codes", align_bytes=64)
        h = keep.tile([P, PACK, V], F32, name="h", align_bytes=64)
        x_scale_picked = keep.tile([P, S], U8, name="x_scale_picked", align_bytes=64)
        e_scale_picked = keep.tile([P, S], U8, name="e_scale_picked", align_bytes=64)
        x_scale_placed = keep.tile([P, S], U8, name="x_scale_placed", align_bytes=64)
        e_scale_placed = keep.tile([P, S], U8, name="e_scale_placed", align_bytes=64)
        qp = keep.tile([P, V, PACK], BF16, name="qp", align_bytes=64)
        qp_codes = keep.tile([P, V], U32, name="qp_codes", align_bytes=64)
        qp_scales = keep.tile([P, V], U8, name="qp_scales", align_bytes=64)
        qm_scales = keep.tile([P, V], U8, name="qm_scales", align_bytes=64)

        nc.vector.memset(x_scale_table[0:X_STAGE, :].bitcast(I32), 0)
        nc.vector.memset(e_scale_table[:].bitcast(I32), 0)
        nc.vector.memset(x_scale_placed[:].bitcast(I32), 0)
        nc.vector.memset(e_scale_placed[:].bitcast(I32), 0)

        table_load = keep.tile([P, 1], F32, name="table_load")
        nc.vector.memset(table_load[:], 0.0)
        nc.scalar.activation(table_load[:], table_load[:], ACT.Exp)

        nc.sync.dma_start(offsets[:], offs)
        nc.scalar.dma_start(out=x_scale_table[X_STAGE:P, :].bitcast(I32), in_=x_scales[0].bitcast(I32))
        nc.sync.dma_start(out=h[:], in_=hT.rearrange("(p j) t -> p j t", j=PACK))
        nc.sync.dma_start(out=e_scale_table[E_STAGE : E_STAGE + PACK * BLOCKS : PACK, :].bitcast(I32), in_=e_scales[0].bitcast(I32))
        nc.sync.dma_start(out=x_word_table[:], in_=x_words[0].rearrange("p n t -> p (n t)").bitcast(I32))

        nc.vector.tensor_copy(x_scale_picked[:], x_scale_table[:].indirect(offsets[:]))
        for r in range(PACK):
            queue = nc.sync if r % 2 else nc.scalar
            queue.dma_start(out=x_scale_placed[r:P:GROUP, :].bitcast(I32),
                            in_=x_scale_picked[X_STAGE + r : P : PACK, :].bitcast(I32))
        e_word_table = keep.tile([P, T], I32, name="e_word_table", tag="x_scales_then_e_words", align_bytes=64)
        nc.sync.dma_start(out=e_word_table[:], in_=e_words[0].rearrange("p n t -> p (n t)").bitcast(I32))

        nc.vector.tensor_copy(e_scale_picked[:], e_scale_table[:].indirect(offsets[:]))
        for r in range(PACK):
            queue = nc.sync if r > 1 else nc.gpsimd
            queue.dma_start(out=e_scale_placed[E_ROW + r : P : GROUP, :].bitcast(I32),
                            in_=e_scale_picked[E_STAGE + PACK * r : E_STAGE + PACK * BLOCKS : PACK * PACK, :].bitcast(I32))

        h_walk = h[:].rearrange("p j (c i) -> p c j i", i=PACK)
        nc.scalar.activation(woven(qp[:]), h_walk, ACT.Relu)
        qm_negated = keep.tile([P, V, PACK], BF16, name="qm_negated", tag="e_scales_then_qm", align_bytes=64)
        share = V // 2 // PACK
        nc.vector.tensor_scalar(woven(qm_negated[:])[:, :share], h_walk[:, :share], 0.0, None, ALU.min)
        qm_half = keep.tile([P, V // 2, PACK], BF16, name="qm_half", align_bytes=64)
        nc.scalar.activation(woven(qm_half[:]), h_walk[:, share:], ACT.Relu, scale=-1.0)
        nc.scalar.activation(flat(qm_negated[:, V // 2 :, :]), flat(qm_half[:]), ACT.Copy, scale=-1.0)
        nc.vector.quantize_mx(out=qp_codes[:].bitcast(FP8X4), scales=qp_scales[:], in_=flat(qp[:]))

        x_word_picked = [keep.tile([P, HALF], U32, name=f"x_word_picked{u}", align_bytes=64) for u in range(2)]
        for u in range(2):
            nc.vector.tensor_copy(x_word_picked[u][:], x_word_table[:].bitcast(U32).indirect(offsets[:, 16 * u : 16 * u + 16]))
        qm_codes = keep.tile([P, V], U32, name="qm_codes", tag="x_words_then_qm_codes", align_bytes=64)
        nc.vector.quantize_mx(out=qm_codes[:].bitcast(FP8X4), scales=qm_scales[:], in_=flat(qm_negated[:]))
        e_word_picked = [keep.tile([P, HALF], U32, name=f"e_word_picked{u}", align_bytes=64) for u in range(2)]
        for lo in range(0, S, QUARTER):
            hi = lo + QUARTER
            u = lo // HALF
            nc.vector.tensor_copy(e_word_picked[u][:, lo - u * HALF : hi - u * HALF],
                                  e_word_table[:].bitcast(U32).indirect(offsets[:, lo // 16 : hi // 16]))

        pieces = [(0, 0, HALF), (1, 0, QUARTER), (0, HALF, S), (1, QUARTER, S)]
        y = [psum.tile([P, hi - lo], F32, name=f"y{n}") for n, (b, lo, hi) in enumerate(pieces)]
        passes = [(0, 0, HALF), (1, 0, QUARTER), (3, QUARTER, HALF), (3, HALF, S), (2, HALF, S)]
        for n, lo, hi in passes:
            b, first, last = pieces[n]
            u = lo // HALF
            nc.tensor.matmul_mx(out=y[n][:, lo - first : hi - first], lhsT=qp_codes[:, queries[b]].bitcast(FP8X4),
                                lhsT_scale=qp_scales[:, queries[b]],
                                rhs=x_word_picked[u][:, lo - u * HALF : hi - u * HALF].bitcast(FP8X4),
                                rhs_scale=x_scale_placed[:, lo:hi], start=lo == first, stop=False)
        e_passes = [(0, 0, QUARTER), (0, QUARTER, HALF), (1, 0, QUARTER), (3, QUARTER, HALF),
                    (2, HALF, HALF + QUARTER), (2, HALF + QUARTER, S), (3, HALF, S)]
        for n, lo, hi in e_passes:
            b, first, last = pieces[n]
            u = lo // HALF
            nc.tensor.matmul_mx(out=y[n][:, lo - first : hi - first], lhsT=qm_codes[:, queries[b]].bitcast(FP8X4),
                                lhsT_scale=qm_scales[:, queries[b]],
                                rhs=e_word_picked[u][:, lo - u * HALF : hi - u * HALF].bitcast(FP8X4),
                                rhs_scale=e_scale_placed[E_ROW:P, lo:hi], start=False, stop=hi == last)

        minus_y = [keep.tile([P, S], F32, name=f"minus_y{b}") for b in range(2)]
        minimum = [keep.tile([P, 1], F32, name=f"minimum{n}") for n in range(4)]
        for n, (b, lo, hi) in enumerate(pieces):
            nc.vector.tensor_scalar(minus_y[b][:, lo:hi], y[n][:], -1.0, minimum[n - 2][:] if lo else None,
                                    ALU.mult, ALU.min, accum_out=minimum[n][:])
        for b, rows in enumerate(queries):
            total = keep.tile([P, 1], F32, name=f"total{b}")
            inverse = keep.tile([P, 1], F32, name=f"inverse{b}")
            exps = keep.tile([P, S], F32, name=f"exps{b}")
            nc.scalar.activation(exps[:], minus_y[b][:], ACT.Exp, bias=minimum[2 + b][:], scale=-1.0, accum_out=total[:])
            nc.vector.reciprocal(inverse[:], total[:])
            for u, pages in enumerate([slice(0, QUARTER), slice(QUARTER, S)]):
                result = keep.tile([P, pages.stop - pages.start], F32, name=f"result{b}{u}")
                nc.vector.tensor_scalar(result[:], exps[:, pages], inverse[:], None, ALU.mult)
                nc.sync.dma_start(out=out[rows, pages], in_=result[:])
